import numpy as np, ml_dtypes
CORES = [51,54,179,182]
N = 4
BF = ml_dtypes.bfloat16
def gentries(a):
    return np.ascontiguousarray(a.reshape(8, 16, -1).transpose(0, 2, 1)).reshape(8, -1)
def gtable(e):
    e = np.asarray(e); return np.ascontiguousarray(e.reshape(8, -1, 16).transpose(0, 2, 1)).reshape(128, -1).astype(np.int32)
W, Q, RO, END = 1536, 1536, 4, 2 ** 20 - 1
def rise(rng, n, lo, hi, e):
    return lo + (np.sort(rng.random(n)) ** e * (hi - lo - n)).astype(np.int64) + np.arange(n)
def split(rng, w, total):
    return 1 + rng.multinomial(total - len(w), np.minimum(w * np.reciprocal(np.sum(w)), 1.0))
def families(rng, L, dev, e, total):
    u = np.exp2(dev * rng.standard_normal(L)); nb0 = split(rng, u, total); like = rng.random(L) < 0.6; like[0] = True; like[1] = False
    rest = total - int(np.sum(nb0[like])); m = L - int(np.sum(like)); nb = np.tile(nb0, (N, 1))
    for r in range(N): nb[r, ~like] = split(rng, u[~like] * np.exp2(2 * rng.standard_normal(m)), rest)
    pad = rng.integers(1, 17, (N, L)); top = np.max(16 * nb - pad, axis=0); base = []
    for l in range(L):
        t = int(top[l]); more = (0, 1, t // 16)[int(rng.integers(0, 3))] if like[l] else t // 8
        base.append(rise(rng, max(1, t + more), 0, END, e))
    return nb, pad, base
def lay(rng, nb, pad, base, mode):
    ids = np.full((N, W * 16), END, np.int64); fst = np.zeros(nb.shape, np.int64)
    for r in range(N):
        at = 0
        for l in rng.permutation(nb.shape[1]):
            b = base[l]; n = int(nb[r, l]); c = 16 * n - int(pad[r, l]); fst[r, l] = at
            if c > 0:
                if mode == 1: v = b[len(b) - c:]
                else:
                    ix = np.sort(rng.permutation(len(b))[:c])
                    if mode == 2:
                        ix[-1] = len(b) - 1
                        if c > 1: ix[0] = 0
                    v = b[ix]
                ids[r, 16 * at:16 * at + c] = v
            at += n
    return np.ascontiguousarray(ids.reshape(N, W, 16).transpose(0, 2, 1)), fst
def starts(rng, nb, fst):
    L = nb.shape[1]; f = np.tile(rng.integers(0, L, Q), (N, 1))
    f = np.where((rng.random((N, Q)) < 0.5) & (rng.random(Q) < 0.125), rng.integers(0, L, (N, Q)), f)
    u = np.where(rng.random(Q) < 0.125, rng.random((N, Q)), rng.random(Q) * (rng.random(Q) < 0.5))
    m = np.take_along_axis(nb, f, 1)
    return np.take_along_axis(fst, f, 1) + np.minimum((u * m).astype(np.int64), m - 1)
def follow(a):
    last = np.concatenate([a[..., 15, :], np.full(a.shape[:-2] + (16,), END, a.dtype)], axis=-1)
    t = np.empty(a.shape, a.dtype); t[..., 0, :] = last[..., :W]
    for i in range(1, 16): t[..., i, :] = np.where(t[..., i - 1, :] == END, END, last[..., i:i + W])
    return t
def pack(ids, st):
    a = np.stack(ids, axis=1); s = np.stack(st, axis=1)
    return {"ids": a.reshape(N, 128, W).astype(np.int32), "tops": follow(a).reshape(N, 128, W).astype(np.int32), "st": np.stack([gtable(x) for x in s])}
def setup_inputs(rng):
    ids, st = [], []
    for g in range(8):
        nb, pad, base = families(rng, int(rng.integers(12, 49)), 1.5, 1.0, W)
        a, fst = lay(rng, nb, pad, base, 0); ids.append(a); st.append(starts(rng, nb, fst))
    return pack(ids, st)
def setup_inputs_far(rng):
    ids, st = [], []; dl = np.array([0, 1, 15, 16, 17, 31, 32, 33])
    for g in range(8):
        L = 6; nb = np.tile(63 + split(rng, rng.random(L) + 0.5, W - 63 * L), (N, 1)); pad = np.tile(rng.integers(1, 17, L), (N, 1))
        base = [rise(rng, int(16 * nb[0, l] - pad[0, l]), 0, END, 1.0) for l in range(L)]
        a, fst = lay(rng, nb, pad, base, 0)
        f = rng.integers(0, L, Q); k = 33 + (rng.random(Q) * (nb[0][f] - 34)).astype(np.int64)
        d = dl[rng.integers(0, np.where(rng.random(Q) < 0.75, 4, 8), (N, Q))]; d[:, :8] = dl
        d[rng.integers(0, N, Q), np.arange(Q)] = 0
        ids.append(a); st.append(np.take_along_axis(fst, np.tile(f, (N, 1)), 1) + k - d)
    return pack(ids, st)
def setup_inputs_ends(rng):
    ids, st = [], []
    for g in range(8):
        nb, pad, base = families(rng, W // 16, 2.0, 1.0, W - 5)
        base = [rise(rng, 1, 0, END, 1.0), np.array([END - 1]), np.array([0, END - 1]), np.array([0, int(rng.integers(1, END - 1)), END - 1]), rise(rng, 15, 0, END, 1.0)] + base
        for b in base[4:]:
            b[0] = 0; b[-1] = END - 1
        nb = np.concatenate([np.ones((N, 5), np.int64), nb], axis=1); pad = np.concatenate([np.tile(np.array([16, 15, 14, 13, 1]), (N, 1)), pad], axis=1)
        a, fst = lay(rng, nb, pad, base, 2); L = nb.shape[1]
        f = np.tile(np.where(rng.random(Q) < 0.25, rng.integers(0, 5, Q), rng.integers(0, L, Q)), (N, 1))
        k = np.where(rng.random(Q) < 0.75, rng.integers(0, 3, Q), rng.integers(0, 3, (N, Q)))
        m = np.take_along_axis(nb, f, 1); s = np.take_along_axis(fst, f, 1) + np.where(k == 0, 0, np.maximum(m - k, 0))
        s[:, 0] = 0; s[:, 1] = W - 1
        ids.append(a); st.append(s)
    return pack(ids, st)
def setup_inputs_alike(rng):
    ids, st = [], []
    for g in range(8):
        L = int(rng.integers(8, 21)); nb = np.tile(split(rng, rng.random(L) + 0.2, W), (N, 1)); pad = rng.integers(1, 17, (N, L)); base = []
        for l in range(L):
            b = np.add.accumulate(rng.choice(np.array([1, 1, 1, 1, 2, 5]), int(16 * nb[0, l] - 1)))
            base.append(b - b[-1] + END - 1 if l % 2 == 0 else b - b[0] + int(rng.integers(0, END - int(b[-1] - b[0]))))
        a, fst = lay(rng, nb, pad, base, 1)
        f = rng.integers(0, L, Q); k = (rng.random(Q) * nb[0][f]).astype(np.int64)
        if g % 2 == 1:
            i = rng.integers(0, 3, Q); f = f[i]; k = k[i]
        ids.append(a); st.append(np.take_along_axis(fst, np.tile(f, (N, 1)), 1) + k)
    return pack(ids, st)
def marks(rng, n):
    k = np.sort(rng.permutation(n // 16 - 1)[:15]) + 1; i = np.concatenate([np.array([-1]), 16 * k, np.array([n])]); v = []
    for m in range(16):
        p = rise(rng, int(i[m + 1] - i[m] - 1), 65536 * m, 65536 * m + 65535, 1.0)
        if rng.random() < 0.5: p[0] = 65536 * m
        v += [p, np.array([65536 * m + 65535])]
    return np.concatenate(v)[:-1]
def runs(n):
    h = n // 16 + 1
    return np.concatenate([np.arange(65536 * m - h // 2, 65536 * m - h // 2 + h) for m in range(1, 16)] + [np.arange(END - h, END)])
def setup_inputs_cases(rng):
    ids, st = [], []; L = 6; al = np.arange(L); aq = np.arange(Q); kinds = rng.permutation(8)
    for g in range(8):
        z = int(kinds[g]); nb = np.tile(63 + split(rng, rng.random(L) + 0.5, W - 63 * L), (N, 1)); m = nb[0]
        pad = np.tile(rng.integers(1, 17, L), (N, 1)); q = rng.integers(0, N, L); add = np.zeros((N, L), np.int64)
        if z == 0:
            add = 65536 * np.stack([rng.permutation(8)[:N] for l in range(L)], axis=1); add[:, 0] = 0; add[q[0], 0] = 65536
        if z == 2:
            add[:] = 1; add[q, al] = 0
        if z == 3:
            pad[:, :3] = 1; pad[q[:3], al[:3]] = 16; pad[:, 3:] = 16; add[q[3:], al[3:]] = 2 ** 19
        base = []
        for l in range(L):
            c = int(16 * m[l] - np.min(pad[:, l]))
            if z == 0: base.append(rise(rng, c, 0, 2 ** 19, 1.0))
            elif z == 1: base.append(marks(rng, c))
            elif z == 2: base.append(rise(rng, c, 1000100, END - 1, 1.0))
            elif z == 3 and l >= 3: base.append(rise(rng, c, 0, 2 ** 18, 1.0))
            elif z == 7: base.append(runs(c * 9 // 8))
            else: base.append(rise(rng, c, 0, END, 1.0))
        a, fst = lay(rng, nb, pad, base, 0 if z == 7 else 1)
        for r in range(N):
            for l in range(L):
                s = int(fst[r, l]); x = a[r, :, s:s + int(m[l])]
                a[r, :, s:s + int(m[l])] = np.where(x < END, x + add[r, l], END)
        f = rng.integers(0, L, Q); u = rng.random(Q); k = (u * m[f]).astype(np.int64); d = np.zeros((N, Q), np.int64)
        if z == 1:
            mk = np.stack([np.flatnonzero(b % 65536 == 65535) // 16 for b in base]); k = np.where(rng.random(Q) < 0.75, mk[f, rng.integers(0, 15, Q)], k)
        if z == 3:
            e = f >= 3; k = np.where(e, m[f] - 1, 16 + (u * (m[f] - 17)).astype(np.int64))
            d = np.where(rng.random((N, Q)) < 0.5, 15, rng.integers(0, 17, (N, Q))); d[:, :Q // 4] = 15; d = np.where(e, 16, d)
            d[q[f], aq] = np.where(e, k - rng.integers(0, 8, Q), 0)
        if z == 4:
            k = 16 + (u * (m[f] - 18)).astype(np.int64); d[q[0]] = rng.integers(1, 17, Q)
        if z == 5:
            o = rng.permutation(W)[:Q]; f = np.repeat(al, m)[o]; k = (np.arange(W) - np.repeat(np.add.accumulate(m) - m, m))[o]
        if z == 6:
            f[:] = int(np.argmax(fst[0])); k = 16 + (u[0] * (m[f] - 18)).astype(np.int64); d = np.tile(rng.integers(0, 17, (N, 1)), (1, Q)); d[q[0]] = 0
        if z == 7:
            k = np.maximum(k, 1); d = rng.integers(0, 2, (N, Q))
        ids.append(a); st.append(np.take_along_axis(fst, np.tile(f, (N, 1)), 1) + k - d)
    return pack(ids, st)
def setup_inputs_spread(rng):
    ids, st = [], []
    for g in range(8):
        nb, pad, base = families(rng, int(rng.integers(4, 65)), 3.0, float(rng.choice(np.array([1.0, 3.0, 8.0]))), W)
        a, fst = lay(rng, nb, pad, base, 0); s = starts(rng, nb, fst)
        ids.append(a); st.append(np.where(rng.random(Q) < 0.25, rng.integers(0, W, (N, Q)), s))
    return pack(ids, st)
def check_inputs(d):
    bad = []
    for k, lo, hi in (("ids", 0, END), ("st", 0, W - 1)):
        if np.min(d[k]) < lo or np.max(d[k]) > hi: bad.append("range of " + k)
    a = d["ids"].astype(np.int64).reshape(N, 8, 16, W); x, y = a[:, :, :-1], a[:, :, 1:]
    if not np.all((y > x) | ((x == END) & (y == END))): bad.append("order inside a block of ids")
    x, y = a[:, :, 15, :-1], a[:, :, 0, 1:]
    if not np.all((y > x) | (x == END)): bad.append("order from block to block of ids")
    if not np.all(a[:, :, 15, W - 1] == END): bad.append("end of the last list of ids")
    if not np.array_equal(d["tops"].astype(np.int64).reshape(N, 8, 16, W), follow(a)): bad.append("tops")
    return bad
def reference(ids, tops, st):
    a = ids.astype(np.int64).reshape(N, 8, 16, W); t = tops.astype(np.int64).reshape(N, 8, 16, W)
    b = np.stack([gentries(x) for x in st]).astype(np.int64)
    cur = np.take_along_axis(a[:, :, 0], b, 2)
    hits = np.zeros((8, Q), np.int64); total = np.zeros((8, Q), np.int64)
    for rnd in range(RO):
        v = np.max(cur, axis=0); hit = (np.min(cur, axis=0) == v) & (v < END)
        hits = hits + hit; total = total + np.where(hit, v, 0); v = v + hit
        n = np.sum(np.take_along_axis(t, b[:, :, None, :], 3) < v[None, :, None, :], axis=2)
        b = b + n
        x = np.take_along_axis(a, b[:, :, None, :], 3)
        p = np.sum(x < v[None, :, None, :], axis=2)
        cur = np.take_along_axis(x, np.minimum(p, 15)[:, :, None, :], 2)[:, :, 0]
    return {"yh": np.stack([gtable(hits)] * N).astype(np.float32), "ys": np.stack([gtable(total)] * N).astype(np.float32),
            "yb": np.stack([gtable(x) for x in b]).astype(np.float32), "yc": np.stack([gtable(x) for x in cur]).astype(np.float32)}

@@ -1,0 +1,363 @@
+import numpy as np
+from concourse.bass import DstId, RemoteDMATransfer
+from concourse.mybir import AluOpType, ActivationFunctionType
+
+CHUNKS = [512, 512, 512]
+RO, NR, W, END = 4, 4, 1536, 2 ** 20 - 1
+NC = len(CHUNKS)
+SIZES = sorted(set(CHUNKS))
+
+SCRATCH = {
+    "x0": ("sbuf", [128, W], "int32"), "tt": ("sbuf", [128, W], "int32"), "ta": ("sbuf", [128, W], "int32"),
+    "ti": ("sbuf", [128, W], "int32"), "td": ("sbuf", [128, W], "float32"), "stb": ("sbuf", [128, W // 16], "int32"),
+    "indb": ("sbuf", [128, 8], "bfloat16"), "indf": ("sbuf", [128, 8], "float32"),
+    "eyeb": ("sbuf", [128, 128], "bfloat16"), "eyef": ("sbuf", [128, 128], "float32"),
+    "sr": ("sbuf", [128, 2048], "bfloat16"),
+    "oh": ("sbuf", [128, W // 16], "float32"), "os_": ("sbuf", [128, W // 16], "float32"),
+    "ob": ("sbuf", [128, W // 16], "float32"), "oc": ("sbuf", [128, W // 16], "float32"),
+}
+for _n in SIZES:
+    SCRATCH["bs%d" % _n] = ("sbuf", [128, _n // 16], "bfloat16")
+    SCRATCH["bc%d" % _n] = ("sbuf", [128, _n], "bfloat16")
+    SCRATCH["cv%d" % _n] = ("sbuf", [128, 128 * (2048 // _n)], "float32")
+for _q in range(NC):
+    _n = CHUNKS[_q]
+    _w = _n // 16
+    for _k, _s, _d in (("off", [128, _w], "uint16"), ("bf", [128, _w], "float16"), ("rc", [128, RO * NR * _w], "float32"),
+                       ("xx", [128, 2 * _w], "float32"), ("nn", [128, 2 * _w], "float32"), ("mx", [128, RO, _w], "float32"),
+                       ("mn", [128, _w], "float32"), ("pc", [128, RO, 3 * _w], "float16"), ("lt", [128, 128], "float16"),
+                       ("gt", [128, _n], "float32"), ("cm", [128, _n], "bfloat16"), ("ga", [128, _n], "float32"),
+                       ("gd", [128, _n], "float32"), ("pp", [128, _n], "float32"), ("hv", [128, RO, _w], "float32"),
+                       ("fs", [128, 256], "float32"), ("yl", [128, _w], "float32"), ("ft", [128, 128], "float32")):
+        SCRATCH["%s%d" % (_k, _q)] = ("sbuf", _s, _d)
+    SCRATCH["pv%d" % _q] = ("psum", [128, 512], "float32")
+    SCRATCH["ps%d" % _q] = ("psum", [128, 512], "float32")
+FIN = 2 * NC < 8
+if FIN:
+    SCRATCH["pf"] = ("psum", [128, 512], "float32")
+
+C = 0.00083
+HOP = 0.08
+
+
+def tt(n, both=True):
+    return 0.05 + max(64, n * (2 if both else 1)) * C
+
+
+def cp(n):
+    return 0.05 + max(64, n) * C
+
+
+def pe(k, n, f=1):
+    return k * n * f * C * 0.7
+
+
+def ga(n):
+    return 0.07 + 1.5 * n * C
+
+
+class Plan:
+    pass
+
+
+def build():
+    ops, lastw, readers = [], {}, {}
+
+    def op(queue, sem, cost, emit, reads, writes, ninc=1, lat=0.0, after=()):
+        o = {"n": len(ops), "q": queue, "sem": sem, "cost": cost, "emit": emit, "ninc": ninc, "lat": lat, "deps": set(after)}
+        for t in reads:
+            if t in lastw:
+                o["deps"].add(lastw[t])
+        for t in writes:
+            if t in lastw:
+                o["deps"].add(lastw[t])
+            o["deps"].update(readers.get(t, ()))
+        for t in reads:
+            readers.setdefault(t, set()).add(o["n"])
+        for t in writes:
+            lastw[t] = o["n"]
+            readers[t] = set()
+        o["deps"].discard(o["n"])
+        ops.append(o)
+        return o["n"]
+
+    A = AluOpType
+    CPY = ActivationFunctionType.Copy
+    op("sync", "l_st", 0.1, lambda g, T, x: [g.sync.dma_start(T.stb[:], T.st[:])], [], ["stb"], 16, 2.0)
+    op("vector", "c_x0", cp(W), lambda g, T, x: [g.vector.memset(T.x0[:], 0)], [], ["x0"])
+    op("sync", "l_x0", 0.1, lambda g, T, x: [g.sync.dma_start(T.x0[0:128:16, :], T.ids[0:128:16, :])], [], ["x0"], 16, 2.2)
+    x0z = ops[-1]["deps"]
+    op("scalar", "l_tt", 0.1, lambda g, T, x: [g.scalar.dma_start(T.tt[:], T.tops[:])], [], ["tt"], 16, 4.5, after=tuple(x0z))
+    op("sync", "l_az", 0.1, lambda g, T, x: [g.sync.dma_start(T.ta[0:128:16, :], T.x0[1:128:16, :])], ["x0z"], ["ta0"], 16, 4.0, after=tuple(x0z))
+
+    def la(g, T, x):
+        return [g.sync.dma_start(T.ta[16 * b + 1:16 * b + 16, :], T.ids[16 * b:16 * b + 15, :]) for b in range(8)]
+    op("sync", "l_ta", 0.8, la, [], ["ta1"], 128, 5.0)
+    op("scalar", "l_ti", 0.1, lambda g, T, x: [g.scalar.dma_start(T.ti[:], T.ids[:])], [], ["ti"], 16, 8.0)
+    op("vector", "c_m1", cp(8), lambda g, T, x: [g.vector.memset(T.indb[:], 1.0)], [], ["indb"])
+    op("vector", "c_m2", cp(128), lambda g, T, x: [g.vector.memset(T.eyeb[:], 0.0)], [], ["eyeb"])
+    for n in SIZES:
+        op("vector", "c_m3_%d" % n, cp(n // 16), lambda g, T, x, n=n: [g.vector.memset(T["bs%d" % n][:], 0.0)], [], ["bs%d" % n])
+    op("vector", "c_m4", cp(1024), lambda g, T, x: [g.vector.memset(T.sr[:], 0.0)], [], ["sr"])
+    for n in SIZES:
+        op("vector", "c_m5_%d" % n, cp(2048 * 128 // n), lambda g, T, x, n=n: [g.vector.memset(T["cv%d" % n][:], 0.0)], [], ["cv%d" % n])
+    op("gpsimd", "c_i1", 0.2, lambda g, T, x: [g.affine_select(T.indb[:], T.indb[:], [[-16, 8]], A.is_ge, 0.0, 0, 1)], ["indb"], ["indb"])
+    op("gpsimd", "c_i2", 0.2, lambda g, T, x: [g.affine_select(T.indb[:], T.indb[:], [[16, 8]], A.is_ge, 0.0, 15, -1)], ["indb"], ["indb"])
+    op("gpsimd", "c_ey", 0.4, lambda g, T, x: [g.affine_select(T.eyeb[:], T.eyeb[:], [[-1, 128]], A.not_equal, 1.0, 0, 1)], ["eyeb"], ["eyeb"])
+    for n in SIZES:
+        w = n // 16
+        for pz, val in ((0, 32.0), (1, 32.0), (2, 1.0)):
+            op("gpsimd", "c_b%d_%d" % (pz, n), 0.25, lambda g, T, x, n=n, w=w, pz=pz, val=val: [
+                g.affine_select(T["bs%d" % n][:], T["bs%d" % n][:], [[-1, w]], A.not_equal, val, -w * pz, 1)], ["bs%d" % n], ["bs%d" % n])
+    op("scalar", "c_if", 0.12, lambda g, T, x: [g.scalar.activation(T.indf[:], T.indb[:], CPY, scale=0.03125)], ["indb"], ["indf"])
+
+    def mksr(g, T, x):
+        return [g.scalar.activation(T.sr[:, 128 * r + r:128 * r + 128:16], T.indb[:], CPY) for r in range(16)]
+    op("scalar", "c_sr", 16 * 0.12, mksr, ["indb"], ["sr"], 16)
+    for n in SIZES:
+        def mkbc(g, T, x, n=n):
+            return [g.scalar.activation(T["bc%d" % n][:, i:n:16], T["bs%d" % n][:], CPY) for i in range(16)]
+        op("scalar", "c_bc%d" % n, 16 * 0.14, mkbc, ["bs%d" % n], ["bc%d" % n], 16)
+    op("scalar", "c_ef", 0.2, lambda g, T, x: [g.scalar.activation(T.eyef[:], T.eyeb[:], CPY)], ["eyeb"], ["eyef"])
+    for n in SIZES:
+        def mkcv(g, T, x, n=n):
+            nk, o = n // 128, []
+            for rh in range(16 // nk):
+                for k in range(nk):
+                    o.append(g.scalar.activation(T["cv%d" % n][:, rh * 128 + nk * rh + k:rh * 128 + 128:16], T.eyef[:, 8 * k:8 * k + 8], CPY))
+            return o
+        op("scalar", "c_cv%d" % n, 16 * 0.12, mkcv, ["eyef"], ["cv%d" % n], 16)
+
+    for d in range(3):
+        def dp(g, T, x, d=d):
+            s = slice(512 * d, 512 * d + 512)
+            return [g.vector.tensor_tensor(T.td[:, s], T.ti[:, s], T.ta[:, s], A.subtract)]
+        op("vector", "td%d" % d, tt(512), dp, ["ti", "ta0", "ta1"], ["td%d" % d])
+    TD = ["td0", "td1", "td2"]
+    c0 = 0
+    for q in range(NC):
+        n = CHUNKS[q]
+        w, nk, rhn = n // 16, n // 128, 16 // (n // 128)
+        S = str(q)
+
+        def B(T, nm, S=S):
+            return T[nm + S]
+
+        def mk(q=q, n=n, w=w, nk=nk, rhn=rhn, S=S, c0=c0):
+            cols = slice(c0, c0 + w)
+            PV, PS = "pv" + S, "ps" + S
+            n_ = ["off", "bf", "gt", "cm", "ga", "gd", "pp", "xx", "nn", "mn", "lt", "hv", "fs", "yl", "ft"]
+            t = dict((k, k + S) for k in n_)
+            op("vector", "of" + S, cp(w), lambda g, T, x: [g.vector.tensor_copy(T[t["off"]][:], T.stb[:, cols])], ["stb"], [t["off"]])
+            op("vector", "bf" + S, cp(w), lambda g, T, x: [g.vector.tensor_copy(T[t["bf"]][:], T.stb[:, cols])], ["stb"], [t["bf"]])
+            if q % 2 == 0:
+                op("scalar", "g0" + S, ga(n), lambda g, T, x: [g.scalar.activation(T[t["pp"]][:], T.x0[:, 0:W].indirect(T[t["off"]][:, 0:w]), CPY)], ["x0", t["off"]], [t["pp"]])
+            else:
+                op("vector", "g0" + S, ga(n), lambda g, T, x: [g.vector.tensor_copy(T[t["pp"]][:], T.x0[:, 0:W].indirect(T[t["off"]][:, 0:w]))], ["x0", t["off"]], [t["pp"]])
+
+            def psum_(g, T, x):
+                return [g.tensor.matmul(T[PS][:, 448 + 8 * k:456 + 8 * k], T[t["pp"]][:, k:n:nk], T.indf[:], True, True) for k in range(nk)]
+
+            def send(r):
+                op("tensor", "ps" + S, pe(nk, 64, 4), psum_, [t["pp"], "indf"], [PS], nk)
+
+                def s1(g, T, x):
+                    o = T["rc" + S][:, (r * NR + x["rank"]) * w:(r * NR + x["rank"] + 1) * w]
+                    i = T[PS][:, 448:448 + w]
+                    if x["rank"] == 1:
+                        return [g.vector.tensor_scalar(o, i, (END - 0.25) / 32.0, None, A.min)]
+                    return [g.vector.tensor_copy(o, i)]
+                op("vector", "s1" + S, cp(w), s1, [], [PS, "own%d_%d" % (q, r)])
+
+                def ex(g, T, x):
+                    s = T["rc" + S][:, (r * NR + x["rank"]) * w:(r * NR + x["rank"] + 1) * w]
+                    tr = [RemoteDMATransfer(dst_ids=[DstId(rid=a[0], pnc=a[1])], dma_engine_mask=m, remote_sem=T.sem["ar%d_%d" % (q, r)],
+                                            srcs=[s], dsts=[s], alu_op=0) for a, m in x["peers"]]
+                    g.remote_dma_fused(tr, local_sem=T.sem["sent"])
+                    return []
+                k = op("gpsimd", None, 1.0, ex, ["own%d_%d" % (q, r)], [], 0)
+                op("remote", "ar%d_%d" % (q, r), 0.0, None, [], ["arr%d_%d" % (q, r)], 0, 2.5, after=(k,))
+
+            send(0)
+            for r in range(RO):
+                op("scalar", "gt" + S, ga(n), lambda g, T, x: [g.scalar.activation(T[t["gt"]][:], T.tt[:, 0:W].indirect(T[t["off"]][:, 0:w]), CPY)], ["tt", t["off"]], [t["gt"]])
+                rc = lambda T, a, b, r=r: T["rc" + S][:, (r * NR + a) * w:(r * NR + b) * w]
+                src = ["arr%d_%d" % (q, r), "own%d_%d" % (q, r)]
+                op("vector", "xx" + S, tt(2 * w), lambda g, T, x, rc=rc: [g.vector.tensor_tensor(T[t["xx"]][:], rc(T, 0, 2), rc(T, 2, 4), A.max)], src, [t["xx"]])
+                op("vector", "nn" + S, tt(2 * w), lambda g, T, x, rc=rc: [g.vector.tensor_tensor(T[t["nn"]][:], rc(T, 0, 2), rc(T, 2, 4), A.min)], src, [t["nn"]])
+                mx = lambda T, r=r: T["mx" + S][:, r, :]
+                pc = lambda T, z, r=r: T["pc" + S][:, r, z * w:z * w + w]
+                half = lambda T, k: (T[t[k]][:, 0:w], T[t[k]][:, w:2 * w])
+                mxt, pct = "mx%s_%d" % (S, r), "pc%s_%d_" % (S, r)
+                op("vector", "mx" + S, tt(w), lambda g, T, x, mx=mx, half=half: [g.vector.tensor_tensor(mx(T), half(T, "xx")[0], half(T, "xx")[1], A.max)], [t["xx"]], [mxt])
+                op("vector", "hi" + S, tt(w), lambda g, T, x, pc=pc, half=half: [g.vector.tensor_tensor(pc(T, 0), half(T, "xx")[0], half(T, "xx")[1], A.max)], [t["xx"]], [pct + "0"])
+                op("vector", "mn" + S, tt(w), lambda g, T, x, half=half: [g.vector.tensor_tensor(T[t["mn"]][:], half(T, "nn")[0], half(T, "nn")[1], A.min)], [t["nn"]], [t["mn"]])
+                op("vector", "lo" + S, tt(w), lambda g, T, x, mx=mx, pc=pc: [g.vector.tensor_tensor(pc(T, 1), mx(T), pc(T, 0), A.subtract)], [mxt, pct + "0"], [pct + "1"])
+                op("vector", "ht" + S, tt(w), lambda g, T, x, mx=mx, pc=pc: [g.vector.tensor_tensor(pc(T, 2), mx(T), T[t["mn"]][:], A.is_equal)], [mxt, t["mn"]], [pct + "2"])
+                op("tensor", "pt" + S, pe(1, 128), lambda g, T, x, r=r: [g.tensor.matmul(T[PS][0:3 * w, 0:128], T["pc" + S][:, r, :], T.eyeb[:], True, True)],
+                   [pct + "0", pct + "1", pct + "2", "eyeb"], [PS])
+                op("vector", "ev" + S, cp(128), lambda g, T, x: [g.vector.tensor_copy(T[t["lt"]][0:3 * w, :], T[PS][0:3 * w, 0:128])], [], [PS, t["lt"]])
+
+                def bc(g, T, x):
+                    return [g.tensor.matmul(T[PV][:, k:n:nk], T["bc%d" % n][0:3 * w, 128 * k:128 * k + 128], T[t["lt"]][0:3 * w, :], True, True) for k in range(nk)]
+                op("tensor", "pb" + S, pe(nk, 128), bc, [t["lt"], "bc%d" % n], [PV], nk)
+                op("vector", "ct" + S, tt(n, False), lambda g, T, x: [g.vector.tensor_tensor(T[t["cm"]][:], T[t["gt"]][:], T[PV][:, 0:n], A.is_lt)], [t["gt"]], [PV, t["cm"]])
+
+                def pn(g, T, x):
+                    o = T[PS][:, 384:384 + w]
+                    return [g.tensor.matmul(o, T.eyeb[:], T[t["bf"]][:], True, False)] + [
+                        g.tensor.matmul(o, T.sr[:, 128 * i:128 * i + 128], T[t["cm"]][:, i:n:16], False, i == 15) for i in range(16)]
+                op("tensor", "pn" + S, pe(17, 64), pn, [t["cm"], t["bf"], "sr", "eyeb"], [PS], 17)
+                op("vector", "of" + S, cp(w), lambda g, T, x: [g.vector.tensor_copy(T[t["off"]][:], T[PS][:, 384:384 + w])], [], [PS, t["off"]])
+                if r < RO - 1:
+                    op("vector", "bf" + S, cp(w), lambda g, T, x: [g.vector.tensor_copy(T[t["bf"]][:], T[PS][:, 384:384 + w])], [], [PS, t["bf"]])
+                else:
+                    op("vector", "bf" + S, cp(w), lambda g, T, x: [g.vector.tensor_copy(T.ob[:, cols], T[PS][:, 384:384 + w])], [], [PS, "ob" + S])
+                op("scalar", "ga" + S, ga(n), lambda g, T, x: [g.scalar.activation(T[t["ga"]][:], T.ta[:, 0:W].indirect(T[t["off"]][:, 0:w]), CPY)], ["ta0", "ta1", t["off"]], [t["ga"]])
+                op("scalar", "gd" + S, ga(n), lambda g, T, x: [g.scalar.activation(T[t["gd"]][:], T.td[:, 0:W].indirect(T[t["off"]][:, 0:w]), CPY)], TD + [t["off"]], [t["gd"]])
+                op("vector", "ca" + S, tt(n, False), lambda g, T, x: [g.vector.tensor_tensor(T[PV][:, 0:n], T[t["ga"]][:], T[PV][:, 0:n], A.is_lt)], [t["ga"]], [PV])
+                op("vector", "mu" + S, tt(n, False), lambda g, T, x: [g.vector.tensor_tensor(T[t["pp"]][:], T[t["gd"]][:], T[PV][:, 0:n], A.mult)], [t["gd"]], [PV, t["pp"]])
+                if r < RO - 1:
+                    send(r + 1)
+            PF = "pf" if FIN else PS
+            fo = 256 if FIN else 384
+            pcs = ["pc%s_%d_2" % (S, r) for r in range(RO)]
+            op("vector", "hv" + S, tt(RO * w), lambda g, T, x: [g.vector.tensor_tensor(T[t["hv"]][:], T["mx" + S][:], T["pc" + S][:, :, 2 * w:3 * w], A.mult)],
+               ["mx%s_%d" % (S, r) for r in range(RO)] + pcs, [t["hv"]])
+
+            def f1(g, T, x):
+                return [g.tensor.matmul(T[PF][0:w, 0:128], T["pc" + S][:, r, 2 * w:3 * w], T.eyeb[:], r == 0, r == RO - 1) for r in range(RO)] + [
+                    g.tensor.matmul(T[PF][0:w, 128:256], T["hv" + S][:, r, :], T.eyef[:], r == 0, r == RO - 1) for r in range(RO)]
+            op("tensor", "f1" + S, pe(20, 128), f1, pcs + [t["hv"], "eyeb", "eyef"], [PF], 8)
+            op("scalar", "f2" + S, 0.3, lambda g, T, x: [g.scalar.activation(T[t["fs"]][0:w, :], T[PF][0:w, 0:256], CPY)], [], [PF, t["fs"]])
+
+            def conv(o, src, m):
+                def f(g, T, x):
+                    return [g.tensor.matmul(o(T), T["cv%d" % n][0:w, 128 * h:128 * h + 128], T[src][0:w, h:m:rhn], h == 0, h == rhn - 1) for h in range(rhn)]
+                return f
+            op("tensor", "f3" + S, pe(rhn, 64, 4), conv(lambda T: T[PF][:, fo:fo + 2 * w], t["fs"], 256), [t["fs"], "cv%d" % n], [PF], rhn)
+            op("scalar", "f4" + S, 0.15, lambda g, T, x: [g.scalar.activation(T.oh[:, cols], T[PF][:, fo:fo + w], CPY)], [], [PF, "oh" + S])
+            op("scalar", "f5" + S, 0.15, lambda g, T, x: [g.scalar.activation(T.os_[:, cols], T[PF][:, fo + w:fo + 2 * w], CPY, scale=32.0)], [], [PF, "os" + S])
+            op("tensor", "ps" + S, pe(nk, 64, 4), psum_, [t["pp"], "indf"], [PS], nk)
+            op("vector", "e1" + S, cp(w), lambda g, T, x: [g.vector.tensor_copy(T[t["yl"]][:], T[PS][:, 448:448 + w])], [], [PS, t["yl"]])
+            op("tensor", "e2" + S, pe(1, 128, 4), lambda g, T, x: [g.tensor.matmul(T[PS][0:w, 256:384], T[t["yl"]][:], T.eyef[:], True, True)], [t["yl"], "eyef"], [PS])
+            op("vector", "e3" + S, cp(128), lambda g, T, x: [g.vector.tensor_copy(T[t["ft"]][0:w, :], T[PS][0:w, 256:384])], [], [PS, t["ft"]])
+            op("tensor", "e4" + S, pe(rhn, 64, 4), conv(lambda T: T[PS][:, 448:448 + w], t["ft"], 128), [t["ft"], "cv%d" % n], [PS], rhn)
+            op("vector", "e5" + S, cp(w), lambda g, T, x: [g.vector.tensor_scalar(T.oc[:, cols], T[PS][:, 448:448 + w], 32.0, None, A.mult)], [], [PS, "oc" + S])
+            for nm, sb, tg in (("yb", "ob", "ob"), ("yh", "oh", "oh"), ("ys", "os_", "os"), ("yc", "oc", "oc")):
+                op("sync", "out", 0.1, lambda g, T, x, nm=nm, sb=sb: [g.sync.dma_start(T[nm][:, cols], T[sb][:, cols])], [tg + S], [], 16, 2.0)
+        mk()
+        c0 += w
+    return ops
+
+
+def schedule(ops):
+    succ = [[] for o in ops]
+    for o in ops:
+        for d in o["deps"]:
+            succ[d].append(o["n"])
+    prio = [0.0] * len(ops)
+    for o in reversed(ops):
+        prio[o["n"]] = o["cost"] + o["lat"] + HOP + max([prio[s] for s in succ[o["n"]]] + [0.0])
+    left = [len(o["deps"]) for o in ops]
+    fin = [0.0] * len(ops)
+    ready = [o["n"] for o in ops if not o["deps"]]
+    free, order = {}, []
+    while ready:
+        best = None
+        for i in ready:
+            o = ops[i]
+            s = max([free.get(o["q"], 0.0) if o["q"] != "remote" else 0.0] + [fin[d] + HOP for d in o["deps"]])
+            key = (round(s, 2), -prio[i], i)
+            if best is None or key < best[0]:
+                best = (key, i, s)
+        k, i, s = best
+        ready.remove(i)
+        o = ops[i]
+        free[o["q"]] = s + o["cost"]
+        fin[i] = s + o["cost"] + o["lat"]
+        order.append(i)
+        for j in succ[i]:
+            left[j] -= 1
+            if left[j] == 0:
+                ready.append(j)
+    return order, fin
+
+
+def plan():
+    ops = build()
+    order, fin = schedule(ops)
+    known, clos, waits, waited = {}, {}, {}, set()
+    for i in order:
+        o = ops[i]
+        q = o["q"]
+        if q == "remote":
+            clos[i] = 1 << i
+            continue
+        k = known.get(q, 0)
+        ws = []
+        for d in sorted(o["deps"], key=lambda d: -fin[d]):
+            if not (k >> d) & 1:
+                if ops[d]["ninc"] == 0 and ops[d]["q"] != "remote":
+                    continue
+                ws.append(d)
+                k |= clos[d]
+        ws = [d for d in ws if not any(e != d and (clos[e] >> d) & 1 for e in ws)]
+        waits[i] = ws
+        waited.update(ws)
+        known[q] = k
+        clos[i] = k | (1 << i)
+    cnt, val, total, semwait = {}, {}, {}, {}
+    for i in order:
+        o = ops[i]
+        if o["q"] != "remote" and o["sem"] is not None and (i in waited or o["sem"] == "out"):
+            cnt[o["sem"]] = cnt.get(o["sem"], 0) + o["ninc"]
+            val[i] = cnt[o["sem"]]
+    return ops, order, waits, val, cnt, fin
+
+
+OPS, ORDER, WAITS, VAL, CNT, FINISH = plan()
+SEMAPHORES = sorted(CNT) + ["ar%d_%d" % (q, r) for q in range(NC) for r in range(RO)] + ["sent"]
+
+
+def rank_program(g, core, T, topo):
+    rank = T.rank_of(core)
+    if rank is None:
+        return
+    peers = [c for c in T.cores if c != core]
+    chip = topo.cores_of(core)
+    far = [c for c in peers if c not in chip]
+    near = [c for c in peers if c in chip]
+    masks = {}
+    used = []
+    for i, c in enumerate(far):
+        e = topo.engines(core, c)
+        e = e[i * (len(e) // len(far)):(i + 1) * (len(e) // len(far))]
+        used += e
+        masks[c] = e
+    for i, c in enumerate(near):
+        e = [k for k in topo.engines(core, c) if k not in used][4 * i:4 * i + 4]
+        masks[c] = e
+    inn = sum(len(masks[c]) for c in peers)
+    x = {"rank": rank, "peers": [(topo.addr(c, core), sum(1 << k for k in masks[c])) for c in far + near]}
+    queue = {"sync": g.sync, "scalar": g.scalar, "vector": g.vector, "tensor": g.tensor, "gpsimd": g}
+    sends = 0
+    for i in ORDER:
+        o = OPS[i]
+        if o["q"] == "remote":
+            continue
+        e = queue[o["q"]]
+        for d in WAITS[i]:
+            p = OPS[d]
+            if p["q"] == "remote":
+                e.wait_ge(T.sem[p["sem"]], inn)
+            else:
+                e.wait_ge(T.sem[p["sem"]], VAL[d])
+        ins = o["emit"](g, T, x)
+        if o["sem"] is None:
+            sends += 1
+        if i in VAL:
+            for k in ins:
+                k.then_inc(T.sem[o["sem"]], o["ninc"] // len(ins))
+    g.sync.wait_ge(T.sem["out"], CNT["out"])
+    g.wait_ge(T.sem["sent"], inn * sends)

@@ -1,70 +1,66 @@
 import numpy as np
 from concourse.bass import DstId, RemoteDMATransfer
-from concourse.mybir import AluOpType, ActivationFunctionType
+from concourse.mybir import AluOpType, ActivationFunctionType, AxisListType
 
 CHUNKS = [512, 512, 512]
 RO, NR, W, END = 4, 4, 1536, 2 ** 20 - 1
-NC = len(CHUNKS)
-SIZES = sorted(set(CHUNKS))
+NC, N = len(CHUNKS), CHUNKS[0]
+L, NK = N // 16, N // 128
+RH = 16 // NK
+SEQ = [
+    1,9,2,3,6,8,4,12,11,14,15,29,7,16,0,40,41,21,28,181,322,323,42,37,182,17,5,43,18,19,20,44,45,46,183,184,185,186,187,32,
+    30,10,22,324,325,326,327,31,38,39,47,329,48,49,50,51,52,53,54,189,188,190,192,55,57,58,328,191,193,330,332,56,59,60,61,
+    194,195,196,197,333,331,334,198,335,336,200,199,337,339,340,201,202,23,63,65,64,67,338,24,25,26,62,204,205,341,342,203,27,
+    66,68,69,70,71,72,73,206,207,208,343,344,345,346,74,75,209,210,212,211,213,214,215,216,347,349,348,350,351,352,353,354,
+    355,356,357,77,78,80,79,81,82,83,84,218,358,219,76,86,87,220,221,222,85,217,88,89,90,92,91,359,223,224,225,361,226,362,
+    93,360,363,364,227,228,229,230,94,95,96,97,231,233,232,234,365,366,98,99,100,368,369,101,102,103,104,367,370,371,235,237,
+    236,238,372,374,375,373,239,241,240,242,376,378,377,379,380,381,382,243,244,383,384,385,386,106,109,108,105,107,110,111,
+    112,114,113,115,116,387,245,247,248,249,250,246,117,118,119,120,121,251,252,253,254,255,388,391,390,256,258,123,124,392,
+    389,393,257,259,122,125,126,394,396,395,260,262,263,127,129,128,130,131,132,133,397,398,399,261,264,266,400,401,404,403,
+    402,265,267,268,269,270,271,272,273,274,405,407,406,408,409,411,410,134,412,413,275,136,158,159,160,414,415,13,34,36,35,
+    135,138,137,139,161,140,141,277,276,278,279,162,163,33,143,142,299,280,281,164,165,416,144,145,146,147,417,282,284,283,
+    420,419,166,167,148,150,421,151,418,422,285,286,287,288,149,423,424,425,152,154,289,291,292,426,427,153,155,156,157,428,
+    429,293,295,169,170,290,294,296,318,300,301,168,440,179,178,171,430,432,431,459,302,303,297,310,298,433,172,173,434,436,
+    435,304,441,443,442,311,312,437,444,174,175,305,438,439,451,452,177,445,176,180,306,313,314,446,447,453,454,455,307,308,
+    309,319,320,448,315,449,450,461,460,456,457,458,462,316,317,321]
 
 SCRATCH = {
-    "x0": ("sbuf", [128, W], "int32"), "tt": ("sbuf", [128, W], "int32"), "ta": ("sbuf", [128, W], "int32"),
-    "ti": ("sbuf", [128, W], "int32"), "td": ("sbuf", [128, W], "float32"), "stb": ("sbuf", [128, W // 16], "int32"),
+    "x0": ("sbuf", [128, W], "int32"), "tt": ("sbuf", [128, W], "int32"), "ti": ("sbuf", [128, W], "int32"),
+    "tb": ("sbuf", [128, W], "float32"), "stb": ("sbuf", [128, W // 16], "int32"),
     "indb": ("sbuf", [128, 8], "bfloat16"), "indf": ("sbuf", [128, 8], "float32"),
+    "sg": ("sbuf", [128, 8], "float32"), "sc": ("sbuf", [128, 1], "float32"), "cab": ("sbuf", [128, 2], "float32"),
     "eyeb": ("sbuf", [128, 128], "bfloat16"), "eyef": ("sbuf", [128, 128], "float32"),
-    "sr": ("sbuf", [128, 2048], "bfloat16"),
-    "oh": ("sbuf", [128, W // 16], "float32"), "os_": ("sbuf", [128, W // 16], "float32"),
+    "dm": ("sbuf", [128, 128], "bfloat16"), "sr": ("sbuf", [128, 2048], "bfloat16"),
+    "bs": ("sbuf", [128, L], "bfloat16"), "bc": ("sbuf", [128, N], "bfloat16"), "cv": ("sbuf", [128, 128 * RH], "bfloat16"),
     "ob": ("sbuf", [128, W // 16], "float32"), "oc": ("sbuf", [128, W // 16], "float32"),
+    "pf0": ("psum", [128, 512], "float32"), "pf1": ("psum", [128, 512], "float32"),
 }
-for _n in SIZES:
-    SCRATCH["bs%d" % _n] = ("sbuf", [128, _n // 16], "bfloat16")
-    SCRATCH["bc%d" % _n] = ("sbuf", [128, _n], "bfloat16")
-    SCRATCH["cv%d" % _n] = ("sbuf", [128, 128 * (2048 // _n)], "float32")
 for _q in range(NC):
-    _n = CHUNKS[_q]
-    _w = _n // 16
-    for _k, _s, _d in (("off", [128, _w], "uint16"), ("bf", [128, _w], "float16"), ("rc", [128, RO * NR * _w], "float32"),
-                       ("xx", [128, 2 * _w], "float32"), ("nn", [128, 2 * _w], "float32"), ("mx", [128, RO, _w], "float32"),
-                       ("mn", [128, _w], "float32"), ("pc", [128, RO, 3 * _w], "float16"), ("lt", [128, 128], "float16"),
-                       ("gt", [128, _n], "float32"), ("cm", [128, _n], "bfloat16"), ("ga", [128, _n], "float32"),
-                       ("gd", [128, _n], "float32"), ("pp", [128, _n], "float32"), ("hv", [128, RO, _w], "float32"),
-                       ("fs", [128, 256], "float32"), ("yl", [128, _w], "float32"), ("ft", [128, 128], "float32")):
+    for _k, _s, _d in (("off", [128, L], "uint16"), ("rc", [128, RO * NR * L], "float32"),
+                       ("xx", [128, 2 * L], "float32"), ("mx", [128, RO * L], "float32"), ("pc", [128, RO, 5 * L], "float16"),
+                       ("lt", [128, 128], "float16"), ("gt", [128, N], "float32"), ("cm", [128, N], "bfloat16"),
+                       ("ga", [128, N], "float32"), ("cc", [128, N], "bfloat16"), ("pp", [128, N], "float32"),
+                       ("hh", [128, RO * L], "bfloat16"), ("hf", [128, RO * L], "float32"), ("hv", [128, RO * L], "float32"),
+                       ("hp", [128, 2 * L], "float16"), ("fs", [128, 128], "float16"), ("oo", [128, 2 * L], "float32"),
+                       ("yp", [128, 2 * L], "float16"), ("ft", [128, 128], "float16")):
         SCRATCH["%s%d" % (_k, _q)] = ("sbuf", _s, _d)
     SCRATCH["pv%d" % _q] = ("psum", [128, 512], "float32")
-    SCRATCH["ps%d" % _q] = ("psum", [128, 512], "float32")
-FIN = 2 * NC < 8
-if FIN:
-    SCRATCH["pf"] = ("psum", [128, 512], "float32")
+    SCRATCH["po%d" % _q] = ("psum", [128, 512], "float32")
 
-C = 0.00083
-HOP = 0.08
-
-
-def tt(n, both=True):
-    return 0.05 + max(64, n * (2 if both else 1)) * C
-
-
-def cp(n):
-    return 0.05 + max(64, n) * C
-
-
-def pe(k, n, f=1):
-    return k * n * f * C * 0.7
-
-
-def ga(n):
-    return 0.07 + 1.5 * n * C
-
-
-class Plan:
-    pass
+SHARE = {"ct0": "va", "ca0": "va", "mu0": "va", "ct1": "vb", "ca1": "vb", "mu1": "vb", "pn0": "ta", "dd0": "ta", "ps0": "ta",
+         "pn1": "tc", "dd1": "tc", "ps1": "tc", "pt": "tp", "pb": "tp", "e3": "tp", "e5": "tp", "xx": "vx", "lo": "vx", "s0": "vx",
+         "ev": "vo", "of": "vo", "e1": "vo", "e2": "vo", "e4": "vo", "e6": "vo", "hv": "vh", "hp": "vh", "hr": "vh", "h2": "vh",
+         "sn": "th", "hs": "th", "h1": "th", "h3": "th", "hf": "sh", "hh": "sh", "h4": "sh"}
 
 
 def build():
-    ops, lastw, readers = [], {}, {}
+    ops, lastw, readers, bank = [], {}, {}, {}
 
-    def op(queue, sem, cost, emit, reads, writes, ninc=1, lat=0.0, after=()):
-        o = {"n": len(ops), "q": queue, "sem": sem, "cost": cost, "emit": emit, "ninc": ninc, "lat": lat, "deps": set(after)}
+    def op(queue, sem, emit, reads, writes, ninc=1, after=(), banks=(), order=(), only=None):
+        n = len(ops)
+        if sem is not None and sem[:-1] in SHARE:
+            sem = SHARE[sem[:-1]] + sem[-1]
+        o = {"n": n, "q": queue, "sem": sem, "emit": emit, "ninc": ninc, "deps": set(after), "order": set(order), "only": only}
         for t in reads:
             if t in lastw:
                 o["deps"].add(lastw[t])
@@ -73,220 +69,234 @@ def build():
                 o["deps"].add(lastw[t])
             o["deps"].update(readers.get(t, ()))
         for t in reads:
-            readers.setdefault(t, set()).add(o["n"])
+            readers.setdefault(t, set()).add(n)
         for t in writes:
-            lastw[t] = o["n"]
+            lastw[t] = n
             readers[t] = set()
-        o["deps"].discard(o["n"])
+        for b in banks:
+            acc = bank.get(b, [])
+            o["deps"].update(i for i in acc if ops[i]["q"] != queue)
+            o["order"].update(i for i in acc if ops[i]["q"] == queue)
+            bank[b] = (acc if any(ops[i]["q"] == queue for i in acc) else []) + [n]
+        o["deps"].discard(n)
+        o["order"] -= o["deps"]
         ops.append(o)
-        return o["n"]
+        return n
 
     A = AluOpType
-    CPY = ActivationFunctionType.Copy
-    op("sync", "l_st", 0.1, lambda g, T, x: [g.sync.dma_start(T.stb[:], T.st[:])], [], ["stb"], 16, 2.0)
-    op("vector", "c_x0", cp(W), lambda g, T, x: [g.vector.memset(T.x0[:], 0)], [], ["x0"])
-    op("sync", "l_x0", 0.1, lambda g, T, x: [g.sync.dma_start(T.x0[0:128:16, :], T.ids[0:128:16, :])], [], ["x0"], 16, 2.2)
-    x0z = ops[-1]["deps"]
-    op("scalar", "l_tt", 0.1, lambda g, T, x: [g.scalar.dma_start(T.tt[:], T.tops[:])], [], ["tt"], 16, 4.5, after=tuple(x0z))
-    op("sync", "l_az", 0.1, lambda g, T, x: [g.sync.dma_start(T.ta[0:128:16, :], T.x0[1:128:16, :])], ["x0z"], ["ta0"], 16, 4.0, after=tuple(x0z))
+    F = ActivationFunctionType
+    CPY = F.Copy
+    V, S, P, G = "vector", "scalar", "tensor", "gpsimd"
+    op("sync", "l_st", lambda g, T, x: [g.sync.dma_start(T.stb[:], T.st[:])], [], ["stb"], 16)
+    za = op(V, "c_x0", lambda g, T, x: [g.vector.memset(T.x0[:, 0:960], 0)], [], [])
+    zb = op(G, "c_x1", lambda g, T, x: [g.iota(T.x0[:, 960:W], [[0, W - 960]], 0, 0)], [], [])
+    l0 = op("sync", "l_x0", lambda g, T, x: [g.sync.dma_start(T.x0[0:128:16, :], T.ids[0:128:16, :])], [], ["x0"], 16, after=(za, zb))
+    l1 = op("sync", "l_ti", lambda g, T, x: [g.sync.dma_start(T.ti[:], T.ids[:])], [], ["ti"], 16, order=(l0,))
+    op("sync", "l_tt", lambda g, T, x: [g.sync.dma_start(T.tt[:], T.tops[:])], [], ["tt"], 16, order=(l1,))
+    op(V, "c_m1", lambda g, T, x: [g.vector.memset(T.indb[:], 1.0)], [], ["indb"])
+    op(V, "c_m2", lambda g, T, x: [g.vector.memset(T.eyeb[:], 0.0)], [], ["eyeb"])
+    op(V, "c_m3", lambda g, T, x: [g.vector.memset(T.bs[:], 0.0)], [], ["bs"])
+    op(V, "c_m4", lambda g, T, x: [g.vector.memset(T.sr[:], 0.0)], [], ["sr"])
+    op(V, "c_m5", lambda g, T, x: [g.vector.memset(T.dm[:], 0.0)], [], ["dm"])
+    op(V, "c_m6", lambda g, T, x: [g.vector.memset(T.sg[:], 1.0)], [], ["sg"])
+    op(V, "c_m7", lambda g, T, x: [g.vector.memset(T.cab[0:64, 0:1], 1.0), g.vector.memset(T.cab[64:128, 0:1], -0.3125),
+                                   g.vector.memset(T.cab[0:64, 1:2], 0.0), g.vector.memset(T.cab[64:128, 1:2], 0.125)], [], ["cab"], 4)
+    op(V, "c_m11", lambda g, T, x: [g.vector.memset(T.cv[:], 0.0)], [], ["cv"])
 
-    def la(g, T, x):
-        return [g.sync.dma_start(T.ta[16 * b + 1:16 * b + 16, :], T.ids[16 * b:16 * b + 15, :]) for b in range(8)]
-    op("sync", "l_ta", 0.8, la, [], ["ta1"], 128, 5.0)
-    op("scalar", "l_ti", 0.1, lambda g, T, x: [g.scalar.dma_start(T.ti[:], T.ids[:])], [], ["ti"], 16, 8.0)
-    op("vector", "c_m1", cp(8), lambda g, T, x: [g.vector.memset(T.indb[:], 1.0)], [], ["indb"])
-    op("vector", "c_m2", cp(128), lambda g, T, x: [g.vector.memset(T.eyeb[:], 0.0)], [], ["eyeb"])
-    for n in SIZES:
-        op("vector", "c_m3_%d" % n, cp(n // 16), lambda g, T, x, n=n: [g.vector.memset(T["bs%d" % n][:], 0.0)], [], ["bs%d" % n])
-    op("vector", "c_m4", cp(1024), lambda g, T, x: [g.vector.memset(T.sr[:], 0.0)], [], ["sr"])
-    for n in SIZES:
-        op("vector", "c_m5_%d" % n, cp(2048 * 128 // n), lambda g, T, x, n=n: [g.vector.memset(T["cv%d" % n][:], 0.0)], [], ["cv%d" % n])
-    op("gpsimd", "c_i1", 0.2, lambda g, T, x: [g.affine_select(T.indb[:], T.indb[:], [[-16, 8]], A.is_ge, 0.0, 0, 1)], ["indb"], ["indb"])
-    op("gpsimd", "c_i2", 0.2, lambda g, T, x: [g.affine_select(T.indb[:], T.indb[:], [[16, 8]], A.is_ge, 0.0, 15, -1)], ["indb"], ["indb"])
-    op("gpsimd", "c_ey", 0.4, lambda g, T, x: [g.affine_select(T.eyeb[:], T.eyeb[:], [[-1, 128]], A.not_equal, 1.0, 0, 1)], ["eyeb"], ["eyeb"])
-    for n in SIZES:
-        w = n // 16
-        for pz, val in ((0, 32.0), (1, 32.0), (2, 1.0)):
-            op("gpsimd", "c_b%d_%d" % (pz, n), 0.25, lambda g, T, x, n=n, w=w, pz=pz, val=val: [
-                g.affine_select(T["bs%d" % n][:], T["bs%d" % n][:], [[-1, w]], A.not_equal, val, -w * pz, 1)], ["bs%d" % n], ["bs%d" % n])
-    op("scalar", "c_if", 0.12, lambda g, T, x: [g.scalar.activation(T.indf[:], T.indb[:], CPY, scale=0.03125)], ["indb"], ["indf"])
+    def sel(name, buf, sl, pat, cmp, fill, base, cm=1):
+        op(G, name, lambda g, T, x: [g.affine_select(T[buf][:, sl], T[buf][:, sl], pat, cmp, fill, base, cm)], [buf], [buf])
+    full = slice(0, 8)
+    sel("c_i1", "indb", full, [[-16, 8]], A.is_ge, 0.0, 0)
+    sel("c_i2", "indb", full, [[16, 8]], A.is_ge, 0.0, 15, -1)
+    sel("c_ey", "eyeb", slice(0, 128), [[-1, 128]], A.not_equal, 1.0, 0)
+    for pz in range(128 // L):
+        sel("c_b%d" % pz, "bs", slice(0, L), [[-1, L]], A.not_equal, 32.0 if pz < 2 else 1.0, -L * pz)
+    sel("c_sg", "sg", full, [[-16, 8]], A.not_equal, -1.0, -15)
+    sel("c_d1", "dm", slice(0, 128), [[-1, 128]], A.not_equal, -1.0, 0)
+    sel("c_d2", "dm", slice(0, 128), [[-1, 128]], A.not_equal, 1.0, 1)
+    sel("c_d3", "dm", slice(0, 128, 16), [[-16, 8]], A.not_equal, 0.0, 1)
+    sel("c_d4", "dm", slice(0, 128, 16), [[-16, 8]], A.not_equal, 1.0, -15)
+    sel("c_d5", "dm", slice(15, 128, 16), [[-16, 8]], A.not_equal, 0.0, -15)
+    sel("c_d6", "dm", slice(15, 128, 16), [[-16, 8]], A.not_equal, -1.0, -14)
+    op(V, "c_sc", lambda g, T, x: [g.vector.tensor_reduce(T.sc[:], T.sg[:], AxisListType.X, A.min)], ["sg"], ["sc"])
+    op(S, "c_if", lambda g, T, x: [g.scalar.activation(T.indf[:], T.indb[:], CPY, scale=0.03125)], ["indb"], ["indf"])
 
     def mksr(g, T, x):
         return [g.scalar.activation(T.sr[:, 128 * r + r:128 * r + 128:16], T.indb[:], CPY) for r in range(16)]
-    op("scalar", "c_sr", 16 * 0.12, mksr, ["indb"], ["sr"], 16)
-    for n in SIZES:
-        def mkbc(g, T, x, n=n):
-            return [g.scalar.activation(T["bc%d" % n][:, i:n:16], T["bs%d" % n][:], CPY) for i in range(16)]
-        op("scalar", "c_bc%d" % n, 16 * 0.14, mkbc, ["bs%d" % n], ["bc%d" % n], 16)
-    op("scalar", "c_ef", 0.2, lambda g, T, x: [g.scalar.activation(T.eyef[:], T.eyeb[:], CPY)], ["eyeb"], ["eyef"])
-    for n in SIZES:
-        def mkcv(g, T, x, n=n):
-            nk, o = n // 128, []
-            for rh in range(16 // nk):
-                for k in range(nk):
-                    o.append(g.scalar.activation(T["cv%d" % n][:, rh * 128 + nk * rh + k:rh * 128 + 128:16], T.eyef[:, 8 * k:8 * k + 8], CPY))
-            return o
-        op("scalar", "c_cv%d" % n, 16 * 0.12, mkcv, ["eyef"], ["cv%d" % n], 16)
+    op(S, "c_sr", mksr, ["indb"], ["sr"], 16)
 
-    for d in range(3):
-        def dp(g, T, x, d=d):
-            s = slice(512 * d, 512 * d + 512)
-            return [g.vector.tensor_tensor(T.td[:, s], T.ti[:, s], T.ta[:, s], A.subtract)]
-        op("vector", "td%d" % d, tt(512), dp, ["ti", "ta0", "ta1"], ["td%d" % d])
-    TD = ["td0", "td1", "td2"]
-    c0 = 0
-    for q in range(NC):
-        n = CHUNKS[q]
-        w, nk, rhn = n // 16, n // 128, 16 // (n // 128)
-        S = str(q)
+    def mkbc(g, T, x):
+        return [g.vector.tensor_copy(T.bc[:, i:N:16], T.bs[:]) for i in range(16)]
+    op(V, "c_bc", mkbc, ["bs"], ["bc"], 16)
+    op(S, "c_ef", lambda g, T, x: [g.scalar.activation(T.eyef[:], T.eyeb[:], CPY)], ["eyeb"], ["eyef"])
+    for h in range(RH):
+        def mkcv(g, T, x, h=h):
+            return [g.scalar.activation(T.cv[:, h * 128 + NK * h + k:h * 128 + 128:16], T.bs[:, 8 * k:8 * k + 8], CPY) for k in range(NK)]
+        op(S, "c_cv%d" % h, mkcv, ["bs", "cv"], ["cv_%d" % h], NK)
+    CV = ["cv_%d" % h for h in range(RH)]
+    op(V, "c_ob", lambda g, T, x: [g.vector.tensor_copy(T.ob[:], T.stb[:])], ["stb"], ["ob%d" % q for q in range(NC)])
+    for h in range(2):
+        def mktb(g, T, x, h=h):
+            s = slice(h * W // 2, h * W // 2 + W // 2)
+            return [g.vector.tensor_scalar(T.tb[:, s], T.ti[:, s], END - 0.25, None, A.min)]
+        op(V, "c_t%d" % h, mktb, ["ti"], ["tb%d" % h], only=1)
 
-        def B(T, nm, S=S):
-            return T[nm + S]
+    def chunk(q):
+        cols = slice(L * q, L * q + L)
+        Z = str(q)
+        PV, PO, PF = "pv" + Z, "po" + Z, "pf%d" % (q % 2)
+        H = N // 2
 
-        def mk(q=q, n=n, w=w, nk=nk, rhn=rhn, S=S, c0=c0):
-            cols = slice(c0, c0 + w)
-            PV, PS = "pv" + S, "ps" + S
-            n_ = ["off", "bf", "gt", "cm", "ga", "gd", "pp", "xx", "nn", "mn", "lt", "hv", "fs", "yl", "ft"]
-            t = dict((k, k + S) for k in n_)
-            op("vector", "of" + S, cp(w), lambda g, T, x: [g.vector.tensor_copy(T[t["off"]][:], T.stb[:, cols])], ["stb"], [t["off"]])
-            op("vector", "bf" + S, cp(w), lambda g, T, x: [g.vector.tensor_copy(T[t["bf"]][:], T.stb[:, cols])], ["stb"], [t["bf"]])
-            if q % 2 == 0:
-                op("scalar", "g0" + S, ga(n), lambda g, T, x: [g.scalar.activation(T[t["pp"]][:], T.x0[:, 0:W].indirect(T[t["off"]][:, 0:w]), CPY)], ["x0", t["off"]], [t["pp"]])
+        def nm(*a):
+            return [k + Z for k in a]
+
+        op(V, "of" + Z, lambda g, T, x: [g.vector.tensor_copy(T["off" + Z][:], T.stb[:, cols])], ["stb"], nm("off"))
+        if q % 2 == 0:
+            op(S, "g0" + Z, lambda g, T, x: [g.scalar.activation(T["pp" + Z][:], T.x0[:, 0:W].indirect(T["off" + Z][:, 0:L]), CPY)],
+               ["x0"] + nm("off"), nm("ppA", "ppB"))
+        else:
+            op(V, "g0" + Z, lambda g, T, x: [g.vector.tensor_copy(T["pp" + Z][:], T.x0[:, 0:W].indirect(T["off" + Z][:, 0:L]))],
+               ["x0"] + nm("off"), nm("ppA", "ppB"))
+
+        def sums():
+            for a, t in ((0, "ppA"), (1, "ppB")):
+                def f(g, T, x, a=a):
+                    return [g.tensor.matmul(T[PV][:, 8 * k:8 * k + 8], T["pp" + Z][:, k:N:NK], T.indf[:], True, True) for k in range(a, NK, 2)]
+                op(P, "ps%d" % a + Z, f, nm(t) + ["indf"], [], NK // 2, banks=[PV])
+
+        def rc(T, r, a, b):
+            return T["rc" + Z][:, (r * NR + a) * L:(r * NR + b) * L]
+
+        def send(r):
+            sums()
+
+            def s1(g, T, x):
+                o, i = rc(T, r, x["rank"], x["rank"] + 1), T[PV][:, 0:L]
+                if r > 0:
+                    return [g.scalar.activation(o, i, CPY)]
+                if x["rank"] == 1:
+                    return [g.vector.tensor_scalar(o, i, (END - 0.25) / 32.0, None, A.min)]
+                return [g.vector.tensor_copy(o, i)]
+            if r > 0:
+                op(S, "s1" + Z, s1, [], ["own%d_%d" % (q, r)], banks=[PV])
             else:
-                op("vector", "g0" + S, ga(n), lambda g, T, x: [g.vector.tensor_copy(T[t["pp"]][:], T.x0[:, 0:W].indirect(T[t["off"]][:, 0:w]))], ["x0", t["off"]], [t["pp"]])
+                op(V, "s0" + Z, s1, [], ["own%d_%d" % (q, r)], banks=[PV])
 
-            def psum_(g, T, x):
-                return [g.tensor.matmul(T[PS][:, 448 + 8 * k:456 + 8 * k], T[t["pp"]][:, k:n:nk], T.indf[:], True, True) for k in range(nk)]
+            def ex(g, T, x):
+                s = rc(T, r, x["rank"], x["rank"] + 1)
+                tr = [RemoteDMATransfer(dst_ids=[DstId(rid=a[0], pnc=a[1])], dma_engine_mask=m, remote_sem=T.sem["ar%d_%d" % (q, r)],
+                                        srcs=[s], dsts=[s], alu_op=0) for a, m in x["peers"]]
+                g.remote_dma_fused(tr, local_sem=T.sem["sent"])
+                return []
+            k = op(G, None, ex, ["own%d_%d" % (q, r)], [], 0)
+            op("remote", "ar%d_%d" % (q, r), None, [], ["arr%d_%d" % (q, r)], 0, after=(k,))
 
-            def send(r):
-                op("tensor", "ps" + S, pe(nk, 64, 4), psum_, [t["pp"], "indf"], [PS], nk)
+        send(0)
+        for r in range(RO):
+            op(S, "gt" + Z, lambda g, T, x: [g.scalar.activation(T["gt" + Z][:], T.tt[:, 0:W].indirect(T["off" + Z][:, 0:L]), CPY)],
+               ["tt"] + nm("off"), nm("gt"))
+            src = ["arr%d_%d" % (q, r), "own%d_%d" % (q, r)]
+            mx = lambda T, r=r: T["mx" + Z][:, r * L:r * L + L]
+            pc = lambda T, a, b, r=r: T["pc" + Z][:, r, a * L:b * L]
+            xh = lambda T: (T["xx" + Z][:, 0:L], T["xx" + Z][:, L:2 * L])
+            pt = "pc%d_%d_" % (q, r)
+            op(V, "xx" + Z, lambda g, T, x, r=r: [g.vector.tensor_tensor(T["xx" + Z][:], rc(T, r, 0, 2), rc(T, r, 2, 4), A.max)], src, nm("xx"))
+            op(V, "ne" + Z, lambda g, T, x, r=r, pc=pc: [g.vector.tensor_tensor(pc(T, 2, 5), rc(T, r, 0, 3), rc(T, r, 1, 4), A.not_equal)], src, [pt + "n"])
+            op(V, "mx" + Z, lambda g, T, x, mx=mx: [g.vector.tensor_tensor(mx(T), xh(T)[0], xh(T)[1], A.max)], nm("xx"), ["mx%d_%d" % (q, r)])
+            op(V, "hi" + Z, lambda g, T, x, pc=pc: [g.vector.tensor_tensor(pc(T, 0, 1), xh(T)[0], xh(T)[1], A.max)], nm("xx"), [pt + "h"])
+            op(V, "lo" + Z, lambda g, T, x, mx=mx, pc=pc: [g.vector.tensor_tensor(pc(T, 1, 2), mx(T), pc(T, 0, 1), A.subtract)],
+               ["mx%d_%d" % (q, r), pt + "h"], [pt + "l"])
 
-                def s1(g, T, x):
-                    o = T["rc" + S][:, (r * NR + x["rank"]) * w:(r * NR + x["rank"] + 1) * w]
-                    i = T[PS][:, 448:448 + w]
-                    if x["rank"] == 1:
-                        return [g.vector.tensor_scalar(o, i, (END - 0.25) / 32.0, None, A.min)]
-                    return [g.vector.tensor_copy(o, i)]
-                op("vector", "s1" + S, cp(w), s1, [], [PS, "own%d_%d" % (q, r)])
+            def tp(g, T, x, pc=pc):
+                return [g.tensor.matmul(T[PO][0:3 * L, 0:128], pc(T, 0, 3), T.eyeb[:], True, True),
+                        g.tensor.matmul(T[PO][3 * L:4 * L, 0:128], pc(T, 3, 4), T.eyeb[:], True, False),
+                        g.tensor.matmul(T[PO][3 * L:4 * L, 0:128], pc(T, 4, 5), T.eyeb[:], False, True)]
+            op(P, "pt" + Z, tp, [pt + "h", pt + "l", pt + "n", "eyeb"], [], 3, banks=[PO])
+            op(V, "ev" + Z, lambda g, T, x: [g.vector.tensor_scalar(T["lt" + Z][:], T[PO][:, 0:128], T.cab[:, 0:1], T.cab[:, 1:2], A.mult, A.add)],
+               ["cab"], nm("lt"), banks=[PO])
+            op(P, "pb" + Z, lambda g, T, x: [
+                g.tensor.matmul(T[PV][:, k:N:NK], T.bc[:, 128 * k:128 * k + 128], T["lt" + Z][:], True, True) for k in range(NK)],
+               nm("lt") + ["bc"], [], NK, banks=[PV])
+            pn = lambda T: T[PO][:, 384:384 + L]
+            op(P, "bm" + Z, lambda g, T, x, pn=pn: [g.tensor.matmul(pn(T), T.eyef[:], T.ob[:, cols], True, False)],
+               nm("ob") + ["eyef"], [], banks=[PO])
+            for a in (0, 1):
+                op(V, "ct%d" % a + Z, lambda g, T, x, a=a: [
+                    g.vector.tensor_tensor(T["cm" + Z][:, a:N:2], T["gt" + Z][:, a:N:2], T[PV][:, a:N:2], A.is_lt)], nm("gt"), nm("cm%d" % a), banks=[PV])
+            for a in (0, 1):
+                def cnt(g, T, x, a=a, pn=pn):
+                    return [g.tensor.matmul(pn(T), T.sr[:, 128 * i:128 * i + 128], T["cm" + Z][:, i:N:16], False, i == 15) for i in range(a, 16, 2)]
+                op(P, "pn%d" % a + Z, cnt, nm("cm%d" % a) + ["sr"], [], 8, banks=[PO])
+            op(V, "of" + Z, lambda g, T, x, pn=pn: [g.vector.tensor_copy(T["off" + Z][:], pn(T))], [], nm("off"), banks=[PO])
+            op(S, "ob" + Z, lambda g, T, x, pn=pn: [g.scalar.activation(T.ob[:, cols], pn(T), CPY)], [], nm("ob"), banks=[PO])
+            for a in (0, 1):
+                def gx(g, T, x, a=a, r=r):
+                    t = T.tb if x["rank"] == 1 and r < RO - 1 else T.ti
+                    return [g.scalar.activation(T["ga" + Z][:, a * H:a * H + H], t[:, 0:W].indirect(T["off" + Z][:, a * L // 2:a * L // 2 + L // 2]), CPY, scale=T.sc[:])]
+                op(S, "ga%d" % a + Z, gx, ["tb0", "tb1", "sc"] + nm("off"), nm("ga%d" % a))
+            for a in (0, 1):
+                h = slice(a * H, a * H + H)
+                op(V, "ca%d" % a + Z, lambda g, T, x, h=h: [
+                    g.vector.tensor_tensor(T["cc" + Z][:, h], T["ga" + Z][:, h], T[PV][:, h], A.is_lt)], nm("ga%d" % a), nm("cc%d" % a), banks=[PV])
+                op(P, "dd%d" % a + Z, lambda g, T, x, h=h: [g.tensor.matmul(T[PO][:, h], T.dm[:], T["cc" + Z][:, h], True, True)],
+                   nm("cc%d" % a) + ["dm"], [], banks=[PO])
+            for a, t in ((0, "ppA"), (1, "ppB")):
+                op(V, "mu%d" % a + Z, lambda g, T, x, a=a: [
+                    g.vector.tensor_tensor(T["pp" + Z][:, a:N:2], T["ga" + Z][:, a:N:2], T[PO][:, a:N:2], A.mult)], nm("ga0", "ga1"), nm(t), banks=[PO])
+            if r < RO - 1:
+                send(r + 1)
+        pcs = ["pc%d_%d_n" % (q, r) for r in range(RO)]
 
-                def ex(g, T, x):
-                    s = T["rc" + S][:, (r * NR + x["rank"]) * w:(r * NR + x["rank"] + 1) * w]
-                    tr = [RemoteDMATransfer(dst_ids=[DstId(rid=a[0], pnc=a[1])], dma_engine_mask=m, remote_sem=T.sem["ar%d_%d" % (q, r)],
-                                            srcs=[s], dsts=[s], alu_op=0) for a, m in x["peers"]]
-                    g.remote_dma_fused(tr, local_sem=T.sem["sent"])
-                    return []
-                k = op("gpsimd", None, 1.0, ex, ["own%d_%d" % (q, r)], [], 0)
-                op("remote", "ar%d_%d" % (q, r), 0.0, None, [], ["arr%d_%d" % (q, r)], 0, 2.5, after=(k,))
+        def sn(g, T, x):
+            return [g.tensor.matmul(T[PF][:, r * L:r * L + L], T.eyeb[:], T["pc" + Z][:, r, z * L:z * L + L], z == 2, z == 4)
+                    for r in range(RO) for z in (2, 3, 4)]
+        op(P, "sn" + Z, sn, pcs + ["eyeb"], [], 3 * RO, banks=[PF])
+        op(S, "hf" + Z, lambda g, T, x: [g.scalar.activation(T["hf" + Z][:], T[PF][:, 0:RO * L], F.Relu, bias=0.25, scale=-0.25)], [], nm("hf"), banks=[PF])
+        op(S, "hh" + Z, lambda g, T, x: [g.scalar.activation(T["hh" + Z][:], T["hf" + Z][:], CPY)], nm("hf"), nm("hh"))
+        op(V, "hv" + Z, lambda g, T, x: [g.vector.tensor_tensor(T["hv" + Z][:], T["mx" + Z][:], T["hf" + Z][:], A.mult)],
+           ["mx%d_%d" % (q, r) for r in range(RO)] + nm("hf"), nm("hv"))
 
-            send(0)
-            for r in range(RO):
-                op("scalar", "gt" + S, ga(n), lambda g, T, x: [g.scalar.activation(T[t["gt"]][:], T.tt[:, 0:W].indirect(T[t["off"]][:, 0:w]), CPY)], ["tt", t["off"]], [t["gt"]])
-                rc = lambda T, a, b, r=r: T["rc" + S][:, (r * NR + a) * w:(r * NR + b) * w]
-                src = ["arr%d_%d" % (q, r), "own%d_%d" % (q, r)]
-                op("vector", "xx" + S, tt(2 * w), lambda g, T, x, rc=rc: [g.vector.tensor_tensor(T[t["xx"]][:], rc(T, 0, 2), rc(T, 2, 4), A.max)], src, [t["xx"]])
-                op("vector", "nn" + S, tt(2 * w), lambda g, T, x, rc=rc: [g.vector.tensor_tensor(T[t["nn"]][:], rc(T, 0, 2), rc(T, 2, 4), A.min)], src, [t["nn"]])
-                mx = lambda T, r=r: T["mx" + S][:, r, :]
-                pc = lambda T, z, r=r: T["pc" + S][:, r, z * w:z * w + w]
-                half = lambda T, k: (T[t[k]][:, 0:w], T[t[k]][:, w:2 * w])
-                mxt, pct = "mx%s_%d" % (S, r), "pc%s_%d_" % (S, r)
-                op("vector", "mx" + S, tt(w), lambda g, T, x, mx=mx, half=half: [g.vector.tensor_tensor(mx(T), half(T, "xx")[0], half(T, "xx")[1], A.max)], [t["xx"]], [mxt])
-                op("vector", "hi" + S, tt(w), lambda g, T, x, pc=pc, half=half: [g.vector.tensor_tensor(pc(T, 0), half(T, "xx")[0], half(T, "xx")[1], A.max)], [t["xx"]], [pct + "0"])
-                op("vector", "mn" + S, tt(w), lambda g, T, x, half=half: [g.vector.tensor_tensor(T[t["mn"]][:], half(T, "nn")[0], half(T, "nn")[1], A.min)], [t["nn"]], [t["mn"]])
-                op("vector", "lo" + S, tt(w), lambda g, T, x, mx=mx, pc=pc: [g.vector.tensor_tensor(pc(T, 1), mx(T), pc(T, 0), A.subtract)], [mxt, pct + "0"], [pct + "1"])
-                op("vector", "ht" + S, tt(w), lambda g, T, x, mx=mx, pc=pc: [g.vector.tensor_tensor(pc(T, 2), mx(T), T[t["mn"]][:], A.is_equal)], [mxt, t["mn"]], [pct + "2"])
-                op("tensor", "pt" + S, pe(1, 128), lambda g, T, x, r=r: [g.tensor.matmul(T[PS][0:3 * w, 0:128], T["pc" + S][:, r, :], T.eyeb[:], True, True)],
-                   [pct + "0", pct + "1", pct + "2", "eyeb"], [PS])
-                op("vector", "ev" + S, cp(128), lambda g, T, x: [g.vector.tensor_copy(T[t["lt"]][0:3 * w, :], T[PS][0:3 * w, 0:128])], [], [PS, t["lt"]])
+        def hs(g, T, x):
+            return [g.tensor.matmul(T[PF][:, 128:128 + L], T.eyef[:], T["hv" + Z][:, r * L:r * L + L], r == 0, r == RO - 1) for r in range(RO)]
+        op(P, "hs" + Z, hs, nm("hh", "hv") + ["eyeb", "eyef"], [], RO, banks=[PF])
+        op(V, "hp" + Z, lambda g, T, x: [g.vector.tensor_copy(T["hp" + Z][:, 0:L], T[PF][:, 128:128 + L])], [], nm("hpa"), banks=[PF])
+        op(V, "hr" + Z, lambda g, T, x: [g.vector.tensor_tensor(T["hp" + Z][:, L:2 * L], T[PF][:, 128:128 + L], T["hp" + Z][:, 0:L], A.subtract)],
+           nm("hpa"), nm("hpb"), banks=[PF])
 
-                def bc(g, T, x):
-                    return [g.tensor.matmul(T[PV][:, k:n:nk], T["bc%d" % n][0:3 * w, 128 * k:128 * k + 128], T[t["lt"]][0:3 * w, :], True, True) for k in range(nk)]
-                op("tensor", "pb" + S, pe(nk, 128), bc, [t["lt"], "bc%d" % n], [PV], nk)
-                op("vector", "ct" + S, tt(n, False), lambda g, T, x: [g.vector.tensor_tensor(T[t["cm"]][:], T[t["gt"]][:], T[PV][:, 0:n], A.is_lt)], [t["gt"]], [PV, t["cm"]])
+        def h1(g, T, x):
+            return [g.tensor.matmul(T[PF][0:2 * L, 256:384], T["hp" + Z][:], T.eyeb[:], True, True)] + [
+                g.tensor.matmul(T[PF][2 * L:3 * L, 256:384], T["hh" + Z][:, r * L:r * L + L], T.eyeb[:], r == 0, r == RO - 1) for r in range(RO)]
+        op(P, "h1" + Z, h1, nm("hpa", "hpb", "hh") + ["eyeb"], [], 1 + RO, banks=[PF])
+        op(V, "h2" + Z, lambda g, T, x: [g.vector.tensor_copy(T["fs" + Z][0:3 * L, :], T[PF][0:3 * L, 256:384])], [], nm("fs"), banks=[PF])
 
-                def pn(g, T, x):
-                    o = T[PS][:, 384:384 + w]
-                    return [g.tensor.matmul(o, T.eyeb[:], T[t["bf"]][:], True, False)] + [
-                        g.tensor.matmul(o, T.sr[:, 128 * i:128 * i + 128], T[t["cm"]][:, i:n:16], False, i == 15) for i in range(16)]
-                op("tensor", "pn" + S, pe(17, 64), pn, [t["cm"], t["bf"], "sr", "eyeb"], [PS], 17)
-                op("vector", "of" + S, cp(w), lambda g, T, x: [g.vector.tensor_copy(T[t["off"]][:], T[PS][:, 384:384 + w])], [], [PS, t["off"]])
-                if r < RO - 1:
-                    op("vector", "bf" + S, cp(w), lambda g, T, x: [g.vector.tensor_copy(T[t["bf"]][:], T[PS][:, 384:384 + w])], [], [PS, t["bf"]])
-                else:
-                    op("vector", "bf" + S, cp(w), lambda g, T, x: [g.vector.tensor_copy(T.ob[:, cols], T[PS][:, 384:384 + w])], [], [PS, "ob" + S])
-                op("scalar", "ga" + S, ga(n), lambda g, T, x: [g.scalar.activation(T[t["ga"]][:], T.ta[:, 0:W].indirect(T[t["off"]][:, 0:w]), CPY)], ["ta0", "ta1", t["off"]], [t["ga"]])
-                op("scalar", "gd" + S, ga(n), lambda g, T, x: [g.scalar.activation(T[t["gd"]][:], T.td[:, 0:W].indirect(T[t["off"]][:, 0:w]), CPY)], TD + [t["off"]], [t["gd"]])
-                op("vector", "ca" + S, tt(n, False), lambda g, T, x: [g.vector.tensor_tensor(T[PV][:, 0:n], T[t["ga"]][:], T[PV][:, 0:n], A.is_lt)], [t["ga"]], [PV])
-                op("vector", "mu" + S, tt(n, False), lambda g, T, x: [g.vector.tensor_tensor(T[t["pp"]][:], T[t["gd"]][:], T[PV][:, 0:n], A.mult)], [t["gd"]], [PV, t["pp"]])
-                if r < RO - 1:
-                    send(r + 1)
-            PF = "pf" if FIN else PS
-            fo = 256 if FIN else 384
-            pcs = ["pc%s_%d_2" % (S, r) for r in range(RO)]
-            op("vector", "hv" + S, tt(RO * w), lambda g, T, x: [g.vector.tensor_tensor(T[t["hv"]][:], T["mx" + S][:], T["pc" + S][:, :, 2 * w:3 * w], A.mult)],
-               ["mx%s_%d" % (S, r) for r in range(RO)] + pcs, [t["hv"]])
-
-            def f1(g, T, x):
-                return [g.tensor.matmul(T[PF][0:w, 0:128], T["pc" + S][:, r, 2 * w:3 * w], T.eyeb[:], r == 0, r == RO - 1) for r in range(RO)] + [
-                    g.tensor.matmul(T[PF][0:w, 128:256], T["hv" + S][:, r, :], T.eyef[:], r == 0, r == RO - 1) for r in range(RO)]
-            op("tensor", "f1" + S, pe(20, 128), f1, pcs + [t["hv"], "eyeb", "eyef"], [PF], 8)
-            op("scalar", "f2" + S, 0.3, lambda g, T, x: [g.scalar.activation(T[t["fs"]][0:w, :], T[PF][0:w, 0:256], CPY)], [], [PF, t["fs"]])
-
-            def conv(o, src, m):
-                def f(g, T, x):
-                    return [g.tensor.matmul(o(T), T["cv%d" % n][0:w, 128 * h:128 * h + 128], T[src][0:w, h:m:rhn], h == 0, h == rhn - 1) for h in range(rhn)]
-                return f
-            op("tensor", "f3" + S, pe(rhn, 64, 4), conv(lambda T: T[PF][:, fo:fo + 2 * w], t["fs"], 256), [t["fs"], "cv%d" % n], [PF], rhn)
-            op("scalar", "f4" + S, 0.15, lambda g, T, x: [g.scalar.activation(T.oh[:, cols], T[PF][:, fo:fo + w], CPY)], [], [PF, "oh" + S])
-            op("scalar", "f5" + S, 0.15, lambda g, T, x: [g.scalar.activation(T.os_[:, cols], T[PF][:, fo + w:fo + 2 * w], CPY, scale=32.0)], [], [PF, "os" + S])
-            op("tensor", "ps" + S, pe(nk, 64, 4), psum_, [t["pp"], "indf"], [PS], nk)
-            op("vector", "e1" + S, cp(w), lambda g, T, x: [g.vector.tensor_copy(T[t["yl"]][:], T[PS][:, 448:448 + w])], [], [PS, t["yl"]])
-            op("tensor", "e2" + S, pe(1, 128, 4), lambda g, T, x: [g.tensor.matmul(T[PS][0:w, 256:384], T[t["yl"]][:], T.eyef[:], True, True)], [t["yl"], "eyef"], [PS])
-            op("vector", "e3" + S, cp(128), lambda g, T, x: [g.vector.tensor_copy(T[t["ft"]][0:w, :], T[PS][0:w, 256:384])], [], [PS, t["ft"]])
-            op("tensor", "e4" + S, pe(rhn, 64, 4), conv(lambda T: T[PS][:, 448:448 + w], t["ft"], 128), [t["ft"], "cv%d" % n], [PS], rhn)
-            op("vector", "e5" + S, cp(w), lambda g, T, x: [g.vector.tensor_scalar(T.oc[:, cols], T[PS][:, 448:448 + w], 32.0, None, A.mult)], [], [PS, "oc" + S])
-            for nm, sb, tg in (("yb", "ob", "ob"), ("yh", "oh", "oh"), ("ys", "os_", "os"), ("yc", "oc", "oc")):
-                op("sync", "out", 0.1, lambda g, T, x, nm=nm, sb=sb: [g.sync.dma_start(T[nm][:, cols], T[sb][:, cols])], [tg + S], [], 16, 2.0)
-        mk()
-        c0 += w
+        def conv(o, src, lo, hi):
+            def f(g, T, x):
+                return [g.tensor.matmul(o(T), T.cv[lo:hi, 128 * h:128 * h + 128], T[src][lo:hi, h:128:RH], h == 0, h == RH - 1) for h in range(RH)]
+            return f
+        ca, cb = conv(lambda T: T[PF][:, 384:384 + L], "fs" + Z, 0, 2 * L), conv(lambda T: T[PF][:, 384 + L:384 + 2 * L], "fs" + Z, 2 * L, 3 * L)
+        op(P, "h3" + Z, lambda g, T, x: ca(g, T, x) + cb(g, T, x), nm("fs") + CV, [], 2 * RH, banks=[PF])
+        op(S, "h4" + Z, lambda g, T, x: [g.scalar.activation(T["oo" + Z][:], T[PF][:, 384:384 + 2 * L], CPY, scale=4.0)], [], nm("oo"), banks=[PF])
+        sums()
+        op(V, "e1" + Z, lambda g, T, x: [g.vector.tensor_copy(T["yp" + Z][:, 0:L], T[PV][:, 0:L])], [], nm("ypa"), banks=[PV])
+        op(V, "e2" + Z, lambda g, T, x: [g.vector.tensor_tensor(T["yp" + Z][:, L:2 * L], T[PV][:, 0:L], T["yp" + Z][:, 0:L], A.subtract)],
+           nm("ypa"), nm("ypb"), banks=[PV])
+        op(P, "e3" + Z, lambda g, T, x: [g.tensor.matmul(T[PO][0:2 * L, 0:128], T["yp" + Z][:], T.eyeb[:], True, True)],
+           nm("ypa", "ypb") + ["eyeb"], [], banks=[PO])
+        op(V, "e4" + Z, lambda g, T, x: [g.vector.tensor_copy(T["ft" + Z][0:2 * L, :], T[PO][0:2 * L, 0:128])], [], nm("ft"), banks=[PO])
+        op(P, "e5" + Z, conv(lambda T: T[PO][:, 384:384 + L], "ft" + Z, 0, 2 * L), nm("ft") + CV, [], RH, banks=[PO])
+        op(V, "e6" + Z, lambda g, T, x: [g.vector.tensor_copy(T.oc[:, cols], T[PO][:, 384:384 + L])], [], nm("oc"), banks=[PO])
+        for y, src, tok in (("yb", lambda T: T.ob[:, cols], "ob"), ("ys", lambda T: T["oo" + Z][:, 0:L], "oo"),
+                            ("yh", lambda T: T["oo" + Z][:, L:2 * L], "oo"), ("yc", lambda T: T.oc[:, cols], "oc")):
+            op("sync", "out", lambda g, T, x, y=y, src=src: [g.sync.dma_start(T[y][:, cols], src(T))], nm(tok), [], 16)
+    for q in range(NC):
+        chunk(q)
     return ops
 
 
-def schedule(ops):
-    succ = [[] for o in ops]
-    for o in ops:
-        for d in o["deps"]:
-            succ[d].append(o["n"])
-    prio = [0.0] * len(ops)
-    for o in reversed(ops):
-        prio[o["n"]] = o["cost"] + o["lat"] + HOP + max([prio[s] for s in succ[o["n"]]] + [0.0])
-    left = [len(o["deps"]) for o in ops]
-    fin = [0.0] * len(ops)
-    ready = [o["n"] for o in ops if not o["deps"]]
-    free, order = {}, []
-    while ready:
-        best = None
-        for i in ready:
-            o = ops[i]
-            s = max([free.get(o["q"], 0.0) if o["q"] != "remote" else 0.0] + [fin[d] + HOP for d in o["deps"]])
-            key = (round(s, 2), -prio[i], i)
-            if best is None or key < best[0]:
-                best = (key, i, s)
-        k, i, s = best
-        ready.remove(i)
-        o = ops[i]
-        free[o["q"]] = s + o["cost"]
-        fin[i] = s + o["cost"] + o["lat"]
-        order.append(i)
-        for j in succ[i]:
-            left[j] -= 1
-            if left[j] == 0:
-                ready.append(j)
-    return order, fin
-
-
 def plan():
-    ops = build()
-    order, fin = schedule(ops)
+    ops, order = build(), SEQ
+    pos = {i: z for z, i in enumerate(order)}
+    assert len(pos) == len(ops) and all(pos[d] < pos[o["n"]] for o in ops for d in o["deps"] | o["order"])
     known, clos, waits, waited = {}, {}, {}, set()
     for i in order:
         o = ops[i]
@@ -296,27 +306,33 @@ def plan():
             continue
         k = known.get(q, 0)
         ws = []
-        for d in sorted(o["deps"], key=lambda d: -fin[d]):
-            if not (k >> d) & 1:
+        for d in sorted(o["deps"], key=lambda d: -pos[d]):
+            if o["only"] is not None or not (k >> d) & 1:
                 if ops[d]["ninc"] == 0 and ops[d]["q"] != "remote":
                     continue
                 ws.append(d)
                 k |= clos[d]
-        ws = [d for d in ws if not any(e != d and (clos[e] >> d) & 1 for e in ws)]
+        if o["only"] is None:
+            ws = [d for d in ws if not any(e != d and (clos[e] >> d) & 1 for e in ws)]
         waits[i] = ws
         waited.update(ws)
-        known[q] = k
-        clos[i] = k | (1 << i)
-    cnt, val, total, semwait = {}, {}, {}, {}
+        if o["only"] is None:
+            known[q] = k
+            clos[i] = k | (1 << i)
+        else:
+            clos[i] = 1 << i
+            for d in ws:
+                clos[i] |= clos[d]
+    cnt, val = {}, {}
     for i in order:
         o = ops[i]
         if o["q"] != "remote" and o["sem"] is not None and (i in waited or o["sem"] == "out"):
             cnt[o["sem"]] = cnt.get(o["sem"], 0) + o["ninc"]
             val[i] = cnt[o["sem"]]
-    return ops, order, waits, val, cnt, fin
+    return ops, order, waits, val, cnt
 
 
-OPS, ORDER, WAITS, VAL, CNT, FINISH = plan()
+OPS, ORDER, WAITS, VAL, CNT = plan()
 SEMAPHORES = sorted(CNT) + ["ar%d_%d" % (q, r) for q in range(NC) for r in range(RO)] + ["sent"]
 
 
@@ -341,18 +357,24 @@ def rank_program(g, core, T, topo):
     inn = sum(len(masks[c]) for c in peers)
     x = {"rank": rank, "peers": [(topo.addr(c, core), sum(1 << k for k in masks[c])) for c in far + near]}
     queue = {"sync": g.sync, "scalar": g.scalar, "vector": g.vector, "tensor": g.tensor, "gpsimd": g}
+
+    def wait(e, d):
+        p = OPS[d]
+        if p["only"] not in (None, rank):
+            for k in WAITS[d]:
+                wait(e, k)
+        elif p["q"] == "remote":
+            e.wait_ge(T.sem[p["sem"]], inn)
+        else:
+            e.wait_ge(T.sem[p["sem"]], VAL[d])
     sends = 0
     for i in ORDER:
         o = OPS[i]
-        if o["q"] == "remote":
+        if o["q"] == "remote" or o["only"] not in (None, rank):
             continue
         e = queue[o["q"]]
         for d in WAITS[i]:
-            p = OPS[d]
-            if p["q"] == "remote":
-                e.wait_ge(T.sem[p["sem"]], inn)
-            else:
-                e.wait_ge(T.sem[p["sem"]], VAL[d])
+            wait(e, d)
         ins = o["emit"](g, T, x)
         if o["sem"] is None:
             sends += 1

@@ -7,41 +7,40 @@ RO, NR, W, END = 4, 4, 1536, 2 ** 20 - 1
 NC, N = len(CHUNKS), CHUNKS[0]
 L, NK = N // 16, N // 128
 RH = 16 // NK
+ZV, ZS = 704, 1216
 SEQ = [
-    1,9,2,3,6,8,4,12,11,14,15,29,7,16,0,40,41,21,28,181,322,323,42,37,182,17,5,43,18,19,20,44,45,46,183,184,185,186,187,32,
-    30,10,22,324,325,326,327,31,38,39,47,329,48,49,50,51,52,53,54,189,188,190,192,55,57,58,328,191,193,330,332,56,59,60,61,
-    194,195,196,197,333,331,334,198,335,336,200,199,337,339,340,201,202,23,63,65,64,67,338,24,25,26,62,204,205,341,342,203,27,
-    66,68,69,70,71,72,73,206,207,208,343,344,345,346,74,75,209,210,212,211,213,214,215,216,347,349,348,350,351,352,353,354,
-    355,356,357,77,78,80,79,81,82,83,84,218,358,219,76,86,87,220,221,222,85,217,88,89,90,92,91,359,223,224,225,361,226,362,
-    93,360,363,364,227,228,229,230,94,95,96,97,231,233,232,234,365,366,98,99,100,368,369,101,102,103,104,367,370,371,235,237,
-    236,238,372,374,375,373,239,241,240,242,376,378,377,379,380,381,382,243,244,383,384,385,386,106,109,108,105,107,110,111,
-    112,114,113,115,116,387,245,247,248,249,250,246,117,118,119,120,121,251,252,253,254,255,388,391,390,256,258,123,124,392,
-    389,393,257,259,122,125,126,394,396,395,260,262,263,127,129,128,130,131,132,133,397,398,399,261,264,266,400,401,404,403,
-    402,265,267,268,269,270,271,272,273,274,405,407,406,408,409,411,410,134,412,413,275,136,158,159,160,414,415,13,34,36,35,
-    135,138,137,139,161,140,141,277,276,278,279,162,163,33,143,142,299,280,281,164,165,416,144,145,146,147,417,282,284,283,
-    420,419,166,167,148,150,421,151,418,422,285,286,287,288,149,423,424,425,152,154,289,291,292,426,427,153,155,156,157,428,
-    429,293,295,169,170,290,294,296,318,300,301,168,440,179,178,171,430,432,431,459,302,303,297,310,298,433,172,173,434,436,
-    435,304,441,443,442,311,312,437,444,174,175,305,438,439,451,452,177,445,176,180,306,313,314,446,447,453,454,455,307,308,
-    309,319,320,448,315,449,450,461,460,456,457,458,462,316,317,321]
+    0,4,1,2,8,10,9,12,11,39,301,13,15,170,38,3,5,6,7,16,17,19,20,21,22,23,24,25,31,40,41,42,171,30,43,14,44,302,37,32,177,
+    46,172,303,304,173,174,305,33,175,306,26,18,27,28,29,307,45,176,47,48,50,49,51,178,309,181,312,311,310,180,313,182,179,
+    52,53,308,55,54,314,183,315,34,184,56,57,58,59,185,187,186,316,317,60,61,62,63,188,318,64,66,319,189,190,320,65,67,321,
+    191,192,193,194,322,324,325,323,68,69,195,70,71,196,197,72,326,328,73,198,327,74,329,199,200,330,331,201,202,332,333,
+    203,334,76,77,79,78,204,335,336,205,80,104,81,36,75,206,105,82,106,83,107,84,85,337,108,86,87,88,207,208,209,210,338,
+    211,340,341,339,342,235,212,89,91,213,236,93,237,343,344,92,90,214,215,345,238,216,217,95,347,218,219,94,96,346,35,220,
+    348,97,98,349,350,99,100,222,223,351,221,353,352,354,239,224,226,101,225,102,227,103,355,228,357,229,356,230,358,231,
+    359,360,232,361,362,366,233,363,110,111,112,113,114,109,240,364,234,365,115,367,116,368,117,118,369,119,120,121,122,123,
+    124,125,126,241,243,244,242,372,374,245,375,373,376,127,246,377,128,129,247,378,371,370,248,249,379,130,250,251,131,132,
+    381,382,252,253,380,133,134,383,384,135,254,136,137,255,256,257,258,259,260,261,385,387,388,386,262,389,391,263,264,390,
+    392,393,265,395,394,266,396,267,140,139,141,142,143,397,398,432,144,269,138,145,433,434,399,268,146,435,147,148,149,400,
+    436,271,270,272,273,150,151,443,437,274,401,402,403,404,405,152,153,444,154,438,156,445,439,440,441,275,454,406,276,407,
+    155,277,278,446,408,279,280,158,410,281,282,409,157,159,411,160,161,412,413,162,447,455,283,285,286,414,284,416,417,415,
+    287,163,288,289,290,448,456,164,291,165,418,420,292,449,452,450,451,461,293,166,419,421,457,294,422,424,167,458,423,295,
+    425,296,426,427,297,459,428,298,429,460,168,299,430,169,300,431,442,462,453,463,464]
 
 SCRATCH = {
     "x0": ("sbuf", [128, W], "int32"), "tt": ("sbuf", [128, W], "int32"), "ti": ("sbuf", [128, W], "int32"),
-    "tb": ("sbuf", [128, W], "float32"), "stb": ("sbuf", [128, W // 16], "int32"),
-    "indb": ("sbuf", [128, 8], "bfloat16"), "indf": ("sbuf", [128, 8], "float32"),
-    "sg": ("sbuf", [128, 8], "float32"), "sc": ("sbuf", [128, 1], "float32"), "cab": ("sbuf", [128, 2], "float32"),
-    "eyeb": ("sbuf", [128, 128], "bfloat16"), "eyef": ("sbuf", [128, 128], "float32"),
-    "dm": ("sbuf", [128, 128], "bfloat16"), "sr": ("sbuf", [128, 2048], "bfloat16"),
+    "stb": ("sbuf", [128, W // 16], "int32"), "indb": ("sbuf", [128, 8], "bfloat16"), "indf": ("sbuf", [128, 8], "float32"),
+    "sg": ("sbuf", [128, 8], "float32"), "sc": ("sbuf", [128, 1], "float32"), "cab": ("sbuf", [128, 3], "float32"),
+    "eyeb": ("sbuf", [128, 128], "bfloat16"), "dm": ("sbuf", [128, 128], "bfloat16"), "sr": ("sbuf", [128, 2048], "bfloat16"),
     "bs": ("sbuf", [128, L], "bfloat16"), "bc": ("sbuf", [128, N], "bfloat16"), "cv": ("sbuf", [128, 128 * RH], "bfloat16"),
-    "ob": ("sbuf", [128, W // 16], "float32"), "oc": ("sbuf", [128, W // 16], "float32"),
+    "oh": ("sbuf", [128, W // 16], "float16"), "ob": ("sbuf", [128, W // 16], "float32"), "oc": ("sbuf", [128, W // 16], "float32"),
     "pf0": ("psum", [128, 512], "float32"), "pf1": ("psum", [128, 512], "float32"),
 }
 for _q in range(NC):
     for _k, _s, _d in (("off", [128, L], "uint16"), ("rc", [128, RO * NR * L], "float32"),
-                       ("xx", [128, 2 * L], "float32"), ("mx", [128, RO * L], "float32"), ("pc", [128, RO, 5 * L], "float16"),
+                       ("xx", [128, 2 * L], "float32"), ("mx", [128, L], "float32"), ("pc", [128, RO, 5 * L], "float16"),
                        ("lt", [128, 128], "float16"), ("gt", [128, N], "float32"), ("cm", [128, N], "bfloat16"),
                        ("ga", [128, N], "float32"), ("cc", [128, N], "bfloat16"), ("pp", [128, N], "float32"),
-                       ("hh", [128, RO * L], "bfloat16"), ("hf", [128, RO * L], "float32"), ("hv", [128, RO * L], "float32"),
-                       ("hp", [128, 2 * L], "float16"), ("fs", [128, 128], "float16"), ("oo", [128, 2 * L], "float32"),
+                       ("hf", [128, RO * L], "bfloat16"), ("hv", [128, 2 * RO * L], "float16"), ("fa", [128, 128], "float16"),
+                       ("fb", [128, 256], "float16"), ("oo", [128, 2 * L], "float32"),
                        ("yp", [128, 2 * L], "float16"), ("ft", [128, 128], "float16")):
         SCRATCH["%s%d" % (_k, _q)] = ("sbuf", _s, _d)
     SCRATCH["pv%d" % _q] = ("psum", [128, 512], "float32")
@@ -49,18 +48,18 @@ for _q in range(NC):
 
 SHARE = {"ct0": "va", "ca0": "va", "mu0": "va", "ct1": "vb", "ca1": "vb", "mu1": "vb", "pn0": "ta", "dd0": "ta", "ps0": "ta",
          "pn1": "tc", "dd1": "tc", "ps1": "tc", "pt": "tp", "pb": "tp", "e3": "tp", "e5": "tp", "xx": "vx", "lo": "vx", "s0": "vx",
-         "ev": "vo", "of": "vo", "e1": "vo", "e2": "vo", "e4": "vo", "e6": "vo", "hv": "vh", "hp": "vh", "hr": "vh", "h2": "vh",
-         "sn": "th", "hs": "th", "h1": "th", "h3": "th", "hf": "sh", "hh": "sh", "h4": "sh"}
+         "ev": "so", "of": "so", "ob": "so", "e1": "vo", "e2": "vo", "e6": "vo", "hv": "vh",
+         "sn": "th", "h1": "th", "h3": "th", "hf": "sh", "h2": "sh", "h4": "sh", "e4": "sh"}
 
 
 def build():
     ops, lastw, readers, bank = [], {}, {}, {}
 
-    def op(queue, sem, emit, reads, writes, ninc=1, after=(), banks=(), order=(), only=None):
+    def op(queue, sem, emit, reads, writes, ninc=1, after=(), banks=(), order=()):
         n = len(ops)
         if sem is not None and sem[:-1] in SHARE:
             sem = SHARE[sem[:-1]] + sem[-1]
-        o = {"n": n, "q": queue, "sem": sem, "emit": emit, "ninc": ninc, "deps": set(after), "order": set(order), "only": only}
+        o = {"n": n, "q": queue, "sem": sem, "emit": emit, "ninc": ninc, "deps": set(after), "order": set(order)}
         for t in reads:
             if t in lastw:
                 o["deps"].add(lastw[t])
@@ -87,20 +86,22 @@ def build():
     F = ActivationFunctionType
     CPY = F.Copy
     V, S, P, G = "vector", "scalar", "tensor", "gpsimd"
-    op("sync", "l_st", lambda g, T, x: [g.sync.dma_start(T.stb[:], T.st[:])], [], ["stb"], 16)
-    za = op(V, "c_x0", lambda g, T, x: [g.vector.memset(T.x0[:, 0:960], 0)], [], [])
-    zb = op(G, "c_x1", lambda g, T, x: [g.iota(T.x0[:, 960:W], [[0, W - 960]], 0, 0)], [], [])
-    l0 = op("sync", "l_x0", lambda g, T, x: [g.sync.dma_start(T.x0[0:128:16, :], T.ids[0:128:16, :])], [], ["x0"], 16, after=(za, zb))
-    l1 = op("sync", "l_ti", lambda g, T, x: [g.sync.dma_start(T.ti[:], T.ids[:])], [], ["ti"], 16, order=(l0,))
-    op("sync", "l_tt", lambda g, T, x: [g.sync.dma_start(T.tt[:], T.tops[:])], [], ["tt"], 16, order=(l1,))
+    ls = op("sync", "l_st", lambda g, T, x: [g.sync.dma_start(T.stb[:], T.st[:])], [], ["stb"], 16)
+    zz = op(V, "c_z", lambda g, T, x: [g.vector.memset(T.sr[:, 0:512], 0.0)], [], ["sra"])
+    za = op(V, "c_x0", lambda g, T, x: [g.vector.memset(T.x0[:, 0:ZV], 0)], [], [], order=(zz,))
+    zb = op(S, "c_x1", lambda g, T, x: [g.scalar.activation(T.x0[:, ZV:ZS], T.sr[:, 0:ZS - ZV], CPY)], ["sra"], [])
+    zc = op(G, "c_x2", lambda g, T, x: [g.iota(T.x0[:, ZS:W], [[0, W - ZS]], 0, 0)], [], [])
+    l0 = op("sync", "l_x0", lambda g, T, x: [g.sync.dma_start(T.x0[0:128:16, :], T.ids[0:128:16, :])], [], ["x0"], 16, after=(za, zb, zc), order=(ls,))
+    l1 = op("sync", "l_tt", lambda g, T, x: [g.sync.dma_start(T.tt[:], T.tops[:])], [], ["tt"], 16, order=(l0,))
+    op("sync", "l_ti", lambda g, T, x: [g.sync.dma_start(T.ti[:], T.ids[:])], [], ["ti"], 16, order=(l1,))
     op(V, "c_m1", lambda g, T, x: [g.vector.memset(T.indb[:], 1.0)], [], ["indb"])
     op(V, "c_m2", lambda g, T, x: [g.vector.memset(T.eyeb[:], 0.0)], [], ["eyeb"])
     op(V, "c_m3", lambda g, T, x: [g.vector.memset(T.bs[:], 0.0)], [], ["bs"])
-    op(V, "c_m4", lambda g, T, x: [g.vector.memset(T.sr[:], 0.0)], [], ["sr"])
+    op(V, "c_m4", lambda g, T, x: [g.vector.memset(T.sr[:, 512:2048], 0.0)], [], ["srb"])
     op(V, "c_m5", lambda g, T, x: [g.vector.memset(T.dm[:], 0.0)], [], ["dm"])
     op(V, "c_m6", lambda g, T, x: [g.vector.memset(T.sg[:], 1.0)], [], ["sg"])
-    op(V, "c_m7", lambda g, T, x: [g.vector.memset(T.cab[0:64, 0:1], 1.0), g.vector.memset(T.cab[64:128, 0:1], -0.3125),
-                                   g.vector.memset(T.cab[0:64, 1:2], 0.0), g.vector.memset(T.cab[64:128, 1:2], 0.125)], [], ["cab"], 4)
+    op(V, "c_m7", lambda g, T, x: [g.vector.memset(T.cab[64 * h:64 * h + 64, c:c + 1], v) for h, c, v in (
+        (0, 0, 1.0), (1, 0, -0.3125), (0, 1, 0.0), (1, 1, 0.125), (0, 2, 32.0), (1, 2, 1.0))], [], ["cab"], 6)
     op(V, "c_m11", lambda g, T, x: [g.vector.memset(T.cv[:], 0.0)], [], ["cv"])
 
     def sel(name, buf, sl, pat, cmp, fill, base, cm=1):
@@ -110,7 +111,7 @@ def build():
     sel("c_i2", "indb", full, [[16, 8]], A.is_ge, 0.0, 15, -1)
     sel("c_ey", "eyeb", slice(0, 128), [[-1, 128]], A.not_equal, 1.0, 0)
     for pz in range(128 // L):
-        sel("c_b%d" % pz, "bs", slice(0, L), [[-1, L]], A.not_equal, 32.0 if pz < 2 else 1.0, -L * pz)
+        sel("c_b%d" % pz, "bs", slice(0, L), [[-1, L]], A.not_equal, 1.0, -L * pz)
     sel("c_sg", "sg", full, [[-16, 8]], A.not_equal, -1.0, -15)
     sel("c_d1", "dm", slice(0, 128), [[-1, 128]], A.not_equal, -1.0, 0)
     sel("c_d2", "dm", slice(0, 128), [[-1, 128]], A.not_equal, 1.0, 1)
@@ -123,34 +124,52 @@ def build():
 
     def mksr(g, T, x):
         return [g.scalar.activation(T.sr[:, 128 * r + r:128 * r + 128:16], T.indb[:], CPY) for r in range(16)]
-    op(S, "c_sr", mksr, ["indb"], ["sr"], 16)
+    op(S, "c_sr", mksr, ["indb"], ["sra", "srb"], 16)
 
     def mkbc(g, T, x):
-        return [g.vector.tensor_copy(T.bc[:, i:N:16], T.bs[:]) for i in range(16)]
-    op(V, "c_bc", mkbc, ["bs"], ["bc"], 16)
-    op(S, "c_ef", lambda g, T, x: [g.scalar.activation(T.eyef[:], T.eyeb[:], CPY)], ["eyeb"], ["eyef"])
+        return [g.vector.tensor_scalar(T.bc[:, i:N:16], T.bs[:], T.cab[:, 2:3], None, A.mult) for i in range(16)]
+    op(V, "c_bc", mkbc, ["bs", "cab"], ["bc"], 16)
     for h in range(RH):
         def mkcv(g, T, x, h=h):
             return [g.scalar.activation(T.cv[:, h * 128 + NK * h + k:h * 128 + 128:16], T.bs[:, 8 * k:8 * k + 8], CPY) for k in range(NK)]
         op(S, "c_cv%d" % h, mkcv, ["bs", "cv"], ["cv_%d" % h], NK)
     CV = ["cv_%d" % h for h in range(RH)]
-    op(V, "c_ob", lambda g, T, x: [g.vector.tensor_copy(T.ob[:], T.stb[:])], ["stb"], ["ob%d" % q for q in range(NC)])
-    for h in range(2):
-        def mktb(g, T, x, h=h):
-            s = slice(h * W // 2, h * W // 2 + W // 2)
-            return [g.vector.tensor_scalar(T.tb[:, s], T.ti[:, s], END - 0.25, None, A.min)]
-        op(V, "c_t%d" % h, mktb, ["ti"], ["tb%d" % h], only=1)
+    op(V, "c_ob", lambda g, T, x: [g.vector.tensor_copy(T.oh[:], T.stb[:])], ["stb"], ["oh%d" % q for q in range(NC)])
+
+    def conv(o, parts):
+        def f(g, T, x):
+            steps = [(b, c, n, h) for b, c, n in parts for h in range(RH)]
+            return [g.tensor.matmul(o(T), T.cv[0:n, 128 * h:128 * h + 128], T[b][0:n, c + h:c + 128:RH], i == 0, i == len(steps) - 1)
+                    for i, (b, c, n, h) in enumerate(steps)]
+        return f
+
+    def hits(q, ra, pf):
+        Z = str(q)
+        n = str(ra)
+
+        def sn(g, T, x):
+            return [g.tensor.matmul(T[pf][:, 256 + r * L:256 + r * L + L], T.eyeb[:], T["pc" + Z][:, r, z * L:z * L + L], z == 2, z == 4)
+                    for r in (ra, ra + 1) for z in (2, 3, 4)]
+        op(P, "sn" + Z, sn, ["pc%d_%d_n" % (q, r) for r in (ra, ra + 1)] + ["eyeb"], [], 6, banks=[pf])
+        s = slice(ra * L, ra * L + 2 * L)
+        op(S, "hf" + Z, lambda g, T, x: [g.scalar.activation(T["hf" + Z][:, s], T[pf][:, 256 + ra * L:256 + ra * L + 2 * L], F.Relu, bias=0.25, scale=-0.25)],
+           [], ["hf" + n + Z], banks=[pf])
+
+        def hv(g, T, x):
+            return [g.vector.tensor_tensor(T["hv" + Z][:, (2 * r + a) * L:(2 * r + a) * L + L], T["pc" + Z][:, r, a * L:a * L + L],
+                                           T["hf" + Z][:, r * L:r * L + L], A.mult) for r in (ra, ra + 1) for a in (0, 1)]
+        op(V, "hv" + Z, hv, ["pc%d_%d_%s" % (q, r, t) for r in (ra, ra + 1) for t in "hl"] + ["hf" + n + Z], ["hv" + n + Z], 4)
 
     def chunk(q):
         cols = slice(L * q, L * q + L)
         Z = str(q)
-        PV, PO, PF = "pv" + Z, "po" + Z, "pf%d" % (q % 2)
+        PV, PO = "pv" + Z, "po" + Z
         H = N // 2
 
         def nm(*a):
             return [k + Z for k in a]
 
-        op(V, "of" + Z, lambda g, T, x: [g.vector.tensor_copy(T["off" + Z][:], T.stb[:, cols])], ["stb"], nm("off"))
+        op(V, "oi" + Z, lambda g, T, x: [g.vector.tensor_copy(T["off" + Z][:], T.stb[:, cols])], ["stb"], nm("off"))
         if q % 2 == 0:
             op(S, "g0" + Z, lambda g, T, x: [g.scalar.activation(T["pp" + Z][:], T.x0[:, 0:W].indirect(T["off" + Z][:, 0:L]), CPY)],
                ["x0"] + nm("off"), nm("ppA", "ppB"))
@@ -170,17 +189,12 @@ def build():
         def send(r):
             sums()
 
-            def s1(g, T, x):
+            def s0(g, T, x):
                 o, i = rc(T, r, x["rank"], x["rank"] + 1), T[PV][:, 0:L]
-                if r > 0:
-                    return [g.scalar.activation(o, i, CPY)]
                 if x["rank"] == 1:
                     return [g.vector.tensor_scalar(o, i, (END - 0.25) / 32.0, None, A.min)]
                 return [g.vector.tensor_copy(o, i)]
-            if r > 0:
-                op(S, "s1" + Z, s1, [], ["own%d_%d" % (q, r)], banks=[PV])
-            else:
-                op(V, "s0" + Z, s1, [], ["own%d_%d" % (q, r)], banks=[PV])
+            op(V, "s0" + Z, s0, [], ["own%d_%d" % (q, r)], banks=[PV])
 
             def ex(g, T, x):
                 s = rc(T, r, x["rank"], x["rank"] + 1)
@@ -196,44 +210,44 @@ def build():
             op(S, "gt" + Z, lambda g, T, x: [g.scalar.activation(T["gt" + Z][:], T.tt[:, 0:W].indirect(T["off" + Z][:, 0:L]), CPY)],
                ["tt"] + nm("off"), nm("gt"))
             src = ["arr%d_%d" % (q, r), "own%d_%d" % (q, r)]
-            mx = lambda T, r=r: T["mx" + Z][:, r * L:r * L + L]
+            mx = lambda T: T["mx" + Z][:]
             pc = lambda T, a, b, r=r: T["pc" + Z][:, r, a * L:b * L]
             xh = lambda T: (T["xx" + Z][:, 0:L], T["xx" + Z][:, L:2 * L])
             pt = "pc%d_%d_" % (q, r)
             op(V, "xx" + Z, lambda g, T, x, r=r: [g.vector.tensor_tensor(T["xx" + Z][:], rc(T, r, 0, 2), rc(T, r, 2, 4), A.max)], src, nm("xx"))
             op(V, "ne" + Z, lambda g, T, x, r=r, pc=pc: [g.vector.tensor_tensor(pc(T, 2, 5), rc(T, r, 0, 3), rc(T, r, 1, 4), A.not_equal)], src, [pt + "n"])
-            op(V, "mx" + Z, lambda g, T, x, mx=mx: [g.vector.tensor_tensor(mx(T), xh(T)[0], xh(T)[1], A.max)], nm("xx"), ["mx%d_%d" % (q, r)])
+            op(V, "mx" + Z, lambda g, T, x, mx=mx: [g.vector.tensor_tensor(mx(T), xh(T)[0], xh(T)[1], A.max)], nm("xx"), nm("mx"))
             op(V, "hi" + Z, lambda g, T, x, pc=pc: [g.vector.tensor_tensor(pc(T, 0, 1), xh(T)[0], xh(T)[1], A.max)], nm("xx"), [pt + "h"])
             op(V, "lo" + Z, lambda g, T, x, mx=mx, pc=pc: [g.vector.tensor_tensor(pc(T, 1, 2), mx(T), pc(T, 0, 1), A.subtract)],
-               ["mx%d_%d" % (q, r), pt + "h"], [pt + "l"])
+               nm("mx") + [pt + "h"], [pt + "l"])
 
             def tp(g, T, x, pc=pc):
                 return [g.tensor.matmul(T[PO][0:3 * L, 0:128], pc(T, 0, 3), T.eyeb[:], True, True),
                         g.tensor.matmul(T[PO][3 * L:4 * L, 0:128], pc(T, 3, 4), T.eyeb[:], True, False),
                         g.tensor.matmul(T[PO][3 * L:4 * L, 0:128], pc(T, 4, 5), T.eyeb[:], False, True)]
             op(P, "pt" + Z, tp, [pt + "h", pt + "l", pt + "n", "eyeb"], [], 3, banks=[PO])
-            op(V, "ev" + Z, lambda g, T, x: [g.vector.tensor_scalar(T["lt" + Z][:], T[PO][:, 0:128], T.cab[:, 0:1], T.cab[:, 1:2], A.mult, A.add)],
+            op(S, "ev" + Z, lambda g, T, x: [g.scalar.activation(T["lt" + Z][:], T[PO][:, 0:128], F.Identity, bias=T.cab[:, 1:2], scale=T.cab[:, 0:1])],
                ["cab"], nm("lt"), banks=[PO])
             op(P, "pb" + Z, lambda g, T, x: [
                 g.tensor.matmul(T[PV][:, k:N:NK], T.bc[:, 128 * k:128 * k + 128], T["lt" + Z][:], True, True) for k in range(NK)],
                nm("lt") + ["bc"], [], NK, banks=[PV])
             pn = lambda T: T[PO][:, 384:384 + L]
-            op(P, "bm" + Z, lambda g, T, x, pn=pn: [g.tensor.matmul(pn(T), T.eyef[:], T.ob[:, cols], True, False)],
-               nm("ob") + ["eyef"], [], banks=[PO])
+            op(P, "bm" + Z, lambda g, T, x, pn=pn: [g.tensor.matmul(pn(T), T.eyeb[:], T.oh[:, cols], True, False)],
+               nm("oh") + ["eyeb"], [], banks=[PO])
             for a in (0, 1):
                 op(V, "ct%d" % a + Z, lambda g, T, x, a=a: [
                     g.vector.tensor_tensor(T["cm" + Z][:, a:N:2], T["gt" + Z][:, a:N:2], T[PV][:, a:N:2], A.is_lt)], nm("gt"), nm("cm%d" % a), banks=[PV])
             for a in (0, 1):
                 def cnt(g, T, x, a=a, pn=pn):
                     return [g.tensor.matmul(pn(T), T.sr[:, 128 * i:128 * i + 128], T["cm" + Z][:, i:N:16], False, i == 15) for i in range(a, 16, 2)]
-                op(P, "pn%d" % a + Z, cnt, nm("cm%d" % a) + ["sr"], [], 8, banks=[PO])
-            op(V, "of" + Z, lambda g, T, x, pn=pn: [g.vector.tensor_copy(T["off" + Z][:], pn(T))], [], nm("off"), banks=[PO])
-            op(S, "ob" + Z, lambda g, T, x, pn=pn: [g.scalar.activation(T.ob[:, cols], pn(T), CPY)], [], nm("ob"), banks=[PO])
+                op(P, "pn%d" % a + Z, cnt, nm("cm%d" % a) + ["sra", "srb"], [], 8, banks=[PO])
+            op(S, "of" + Z, lambda g, T, x, pn=pn: [g.scalar.activation(T["off" + Z][:], pn(T), CPY)], [], nm("off"), banks=[PO])
+            to = "oh" if r < RO - 1 else "ob"
+            op(S, "ob" + Z, lambda g, T, x, pn=pn, to=to: [g.scalar.activation(T[to][:, cols], pn(T), CPY)], [], nm(to), banks=[PO])
             for a in (0, 1):
-                def gx(g, T, x, a=a, r=r):
-                    t = T.tb if x["rank"] == 1 and r < RO - 1 else T.ti
-                    return [g.scalar.activation(T["ga" + Z][:, a * H:a * H + H], t[:, 0:W].indirect(T["off" + Z][:, a * L // 2:a * L // 2 + L // 2]), CPY, scale=T.sc[:])]
-                op(S, "ga%d" % a + Z, gx, ["tb0", "tb1", "sc"] + nm("off"), nm("ga%d" % a))
+                def gx(g, T, x, a=a):
+                    return [g.scalar.activation(T["ga" + Z][:, a * H:a * H + H], T.ti[:, 0:W].indirect(T["off" + Z][:, a * L // 2:a * L // 2 + L // 2]), CPY, scale=T.sc[:])]
+                op(S, "ga%d" % a + Z, gx, ["ti", "sc"] + nm("off"), nm("ga%d" % a))
             for a in (0, 1):
                 h = slice(a * H, a * H + H)
                 op(V, "ca%d" % a + Z, lambda g, T, x, h=h: [
@@ -245,51 +259,42 @@ def build():
                     g.vector.tensor_tensor(T["pp" + Z][:, a:N:2], T["ga" + Z][:, a:N:2], T[PO][:, a:N:2], A.mult)], nm("ga0", "ga1"), nm(t), banks=[PO])
             if r < RO - 1:
                 send(r + 1)
-        pcs = ["pc%d_%d_n" % (q, r) for r in range(RO)]
-
-        def sn(g, T, x):
-            return [g.tensor.matmul(T[PF][:, r * L:r * L + L], T.eyeb[:], T["pc" + Z][:, r, z * L:z * L + L], z == 2, z == 4)
-                    for r in range(RO) for z in (2, 3, 4)]
-        op(P, "sn" + Z, sn, pcs + ["eyeb"], [], 3 * RO, banks=[PF])
-        op(S, "hf" + Z, lambda g, T, x: [g.scalar.activation(T["hf" + Z][:], T[PF][:, 0:RO * L], F.Relu, bias=0.25, scale=-0.25)], [], nm("hf"), banks=[PF])
-        op(S, "hh" + Z, lambda g, T, x: [g.scalar.activation(T["hh" + Z][:], T["hf" + Z][:], CPY)], nm("hf"), nm("hh"))
-        op(V, "hv" + Z, lambda g, T, x: [g.vector.tensor_tensor(T["hv" + Z][:], T["mx" + Z][:], T["hf" + Z][:], A.mult)],
-           ["mx%d_%d" % (q, r) for r in range(RO)] + nm("hf"), nm("hv"))
-
-        def hs(g, T, x):
-            return [g.tensor.matmul(T[PF][:, 128:128 + L], T.eyef[:], T["hv" + Z][:, r * L:r * L + L], r == 0, r == RO - 1) for r in range(RO)]
-        op(P, "hs" + Z, hs, nm("hh", "hv") + ["eyeb", "eyef"], [], RO, banks=[PF])
-        op(V, "hp" + Z, lambda g, T, x: [g.vector.tensor_copy(T["hp" + Z][:, 0:L], T[PF][:, 128:128 + L])], [], nm("hpa"), banks=[PF])
-        op(V, "hr" + Z, lambda g, T, x: [g.vector.tensor_tensor(T["hp" + Z][:, L:2 * L], T[PF][:, 128:128 + L], T["hp" + Z][:, 0:L], A.subtract)],
-           nm("hpa"), nm("hpb"), banks=[PF])
-
-        def h1(g, T, x):
-            return [g.tensor.matmul(T[PF][0:2 * L, 256:384], T["hp" + Z][:], T.eyeb[:], True, True)] + [
-                g.tensor.matmul(T[PF][2 * L:3 * L, 256:384], T["hh" + Z][:, r * L:r * L + L], T.eyeb[:], r == 0, r == RO - 1) for r in range(RO)]
-        op(P, "h1" + Z, h1, nm("hpa", "hpb", "hh") + ["eyeb"], [], 1 + RO, banks=[PF])
-        op(V, "h2" + Z, lambda g, T, x: [g.vector.tensor_copy(T["fs" + Z][0:3 * L, :], T[PF][0:3 * L, 256:384])], [], nm("fs"), banks=[PF])
-
-        def conv(o, src, lo, hi):
-            def f(g, T, x):
-                return [g.tensor.matmul(o(T), T.cv[lo:hi, 128 * h:128 * h + 128], T[src][lo:hi, h:128:RH], h == 0, h == RH - 1) for h in range(RH)]
-            return f
-        ca, cb = conv(lambda T: T[PF][:, 384:384 + L], "fs" + Z, 0, 2 * L), conv(lambda T: T[PF][:, 384 + L:384 + 2 * L], "fs" + Z, 2 * L, 3 * L)
-        op(P, "h3" + Z, lambda g, T, x: ca(g, T, x) + cb(g, T, x), nm("fs") + CV, [], 2 * RH, banks=[PF])
-        op(S, "h4" + Z, lambda g, T, x: [g.scalar.activation(T["oo" + Z][:], T[PF][:, 384:384 + 2 * L], CPY, scale=4.0)], [], nm("oo"), banks=[PF])
+            if r == 1:
+                hits(q, 0, "pf0")
+                op(P, "h1" + Z, lambda g, T, x: [g.tensor.matmul(T.pf0[:, 0:128], T["hv" + Z][:, 0:128], T.eyeb[:], True, True)],
+                   nm("hv0") + ["eyeb"], [], banks=["pf0"])
+                op(S, "h2" + Z, lambda g, T, x: [g.scalar.activation(T["fa" + Z][:], T.pf0[:, 0:128], CPY)], [], nm("fa"), banks=["pf0"])
         sums()
         op(V, "e1" + Z, lambda g, T, x: [g.vector.tensor_copy(T["yp" + Z][:, 0:L], T[PV][:, 0:L])], [], nm("ypa"), banks=[PV])
         op(V, "e2" + Z, lambda g, T, x: [g.vector.tensor_tensor(T["yp" + Z][:, L:2 * L], T[PV][:, 0:L], T["yp" + Z][:, 0:L], A.subtract)],
            nm("ypa"), nm("ypb"), banks=[PV])
         op(P, "e3" + Z, lambda g, T, x: [g.tensor.matmul(T[PO][0:2 * L, 0:128], T["yp" + Z][:], T.eyeb[:], True, True)],
            nm("ypa", "ypb") + ["eyeb"], [], banks=[PO])
-        op(V, "e4" + Z, lambda g, T, x: [g.vector.tensor_copy(T["ft" + Z][0:2 * L, :], T[PO][0:2 * L, 0:128])], [], nm("ft"), banks=[PO])
-        op(P, "e5" + Z, conv(lambda T: T[PO][:, 384:384 + L], "ft" + Z, 0, 2 * L), nm("ft") + CV, [], RH, banks=[PO])
-        op(V, "e6" + Z, lambda g, T, x: [g.vector.tensor_copy(T.oc[:, cols], T[PO][:, 384:384 + L])], [], nm("oc"), banks=[PO])
+        op(S, "e4" + Z, lambda g, T, x: [g.scalar.activation(T["ft" + Z][0:2 * L, :], T[PO][0:2 * L, 0:128], CPY)], [], nm("ft"), banks=[PO])
+        op(P, "e5" + Z, conv(lambda T: T[PO][:, 384:384 + L], [("ft" + Z, 0, 2 * L)]), nm("ft") + CV, [], RH, banks=[PO])
+        op(V, "e6" + Z, lambda g, T, x: [g.vector.tensor_scalar(T.oc[:, cols], T[PO][:, 384:384 + L], 32.0, None, A.mult)], [], nm("oc"), banks=[PO])
+
+    def last(q):
+        cols = slice(L * q, L * q + L)
+        Z = str(q)
+        hits(q, 2, "pf0")
+        op(P, "h1" + Z, lambda g, T, x: [g.tensor.matmul(T.pf1[:, 0:128], T["hv" + Z][:, 128:256], T.eyeb[:], True, True),
+                                         g.tensor.matmul(T.pf1[:, 128:256], T["hf" + Z][:], T.eyeb[:], True, True)],
+           ["hv2" + Z, "hf0" + Z, "hf2" + Z, "eyeb"], [], 2, banks=["pf1"])
+        op(S, "h2" + Z, lambda g, T, x: [g.scalar.activation(T["fb" + Z][:], T.pf1[:, 0:256], CPY)], [], ["fb" + Z], banks=["pf1"])
+        c1 = conv(lambda T: T.pf1[:, 384:384 + L], [("fa" + Z, 0, 128), ("fb" + Z, 0, 128)])
+        c2 = conv(lambda T: T.pf1[:, 384 + L:384 + 2 * L], [("fb" + Z, 128, 128)])
+        op(P, "h3" + Z, lambda g, T, x: c1(g, T, x) + c2(g, T, x), ["fa" + Z, "fb" + Z] + CV, [], 3 * RH, banks=["pf1"])
+        op(S, "h4" + Z, lambda g, T, x: [g.scalar.activation(T["oo" + Z][:, 0:L], T.pf1[:, 384:384 + L], CPY, scale=128.0),
+                                         g.scalar.activation(T["oo" + Z][:, L:2 * L], T.pf1[:, 384 + L:384 + 2 * L], CPY, scale=4.0)],
+           [], ["oo" + Z], 2, banks=["pf1"])
         for y, src, tok in (("yb", lambda T: T.ob[:, cols], "ob"), ("ys", lambda T: T["oo" + Z][:, 0:L], "oo"),
                             ("yh", lambda T: T["oo" + Z][:, L:2 * L], "oo"), ("yc", lambda T: T.oc[:, cols], "oc")):
-            op("sync", "out", lambda g, T, x, y=y, src=src: [g.sync.dma_start(T[y][:, cols], src(T))], nm(tok), [], 16)
+            op("sync", "out", lambda g, T, x, y=y, src=src: [g.sync.dma_start(T[y][:, cols], src(T))], [tok + Z], [], 16)
     for q in range(NC):
         chunk(q)
+    for q in range(NC):
+        last(q)
     return ops
 
 
@@ -307,22 +312,16 @@ def plan():
         k = known.get(q, 0)
         ws = []
         for d in sorted(o["deps"], key=lambda d: -pos[d]):
-            if o["only"] is not None or not (k >> d) & 1:
+            if not (k >> d) & 1:
                 if ops[d]["ninc"] == 0 and ops[d]["q"] != "remote":
                     continue
                 ws.append(d)
                 k |= clos[d]
-        if o["only"] is None:
-            ws = [d for d in ws if not any(e != d and (clos[e] >> d) & 1 for e in ws)]
+        ws = [d for d in ws if not any(e != d and (clos[e] >> d) & 1 for e in ws)]
         waits[i] = ws
         waited.update(ws)
-        if o["only"] is None:
-            known[q] = k
-            clos[i] = k | (1 << i)
-        else:
-            clos[i] = 1 << i
-            for d in ws:
-                clos[i] |= clos[d]
+        known[q] = k
+        clos[i] = k | (1 << i)
     cnt, val = {}, {}
     for i in order:
         o = ops[i]
@@ -357,24 +356,15 @@ def rank_program(g, core, T, topo):
     inn = sum(len(masks[c]) for c in peers)
     x = {"rank": rank, "peers": [(topo.addr(c, core), sum(1 << k for k in masks[c])) for c in far + near]}
     queue = {"sync": g.sync, "scalar": g.scalar, "vector": g.vector, "tensor": g.tensor, "gpsimd": g}
-
-    def wait(e, d):
-        p = OPS[d]
-        if p["only"] not in (None, rank):
-            for k in WAITS[d]:
-                wait(e, k)
-        elif p["q"] == "remote":
-            e.wait_ge(T.sem[p["sem"]], inn)
-        else:
-            e.wait_ge(T.sem[p["sem"]], VAL[d])
     sends = 0
     for i in ORDER:
         o = OPS[i]
-        if o["q"] == "remote" or o["only"] not in (None, rank):
+        if o["q"] == "remote":
             continue
         e = queue[o["q"]]
         for d in WAITS[i]:
-            wait(e, d)
+            p = OPS[d]
+            e.wait_ge(T.sem[p["sem"]], inn if p["q"] == "remote" else VAL[d])
         ins = o["emit"](g, T, x)
         if o["sem"] is None:
             sends += 1

import numpy as np
from concourse.bass import DstId, RemoteDMATransfer
from concourse.mybir import AluOpType, ActivationFunctionType, AxisListType

CHUNKS = [512, 512, 512]
RO, NR, W, END = 4, 4, 1536, 2 ** 20 - 1
NC, N = len(CHUNKS), CHUNKS[0]
L, NK = N // 16, N // 128
RH = 16 // NK
ZV, ZS = 704, 1216
SEQ = [
    0,4,1,2,8,10,9,12,11,39,301,13,15,170,38,3,5,6,7,16,17,19,20,21,22,23,24,25,31,40,41,42,171,30,43,14,44,302,37,32,177,
    46,172,303,304,173,174,305,33,175,306,26,18,27,28,29,307,45,176,47,48,50,49,51,178,309,181,312,311,310,180,313,182,179,
    52,53,308,55,54,314,183,315,34,184,56,57,58,59,185,187,186,316,317,60,61,62,63,188,318,64,66,319,189,190,320,65,67,321,
    191,192,193,194,322,324,325,323,68,69,195,70,71,196,197,72,326,328,73,198,327,74,329,199,200,330,331,201,202,332,333,
    203,334,76,77,79,78,204,335,336,205,80,104,81,36,75,206,105,82,106,83,107,84,85,337,108,86,87,88,207,208,209,210,338,
    211,340,341,339,342,235,212,89,91,213,236,93,237,343,344,92,90,214,215,345,238,216,217,95,347,218,219,94,96,346,35,220,
    348,97,98,349,350,99,100,222,223,351,221,353,352,354,239,224,226,101,225,102,227,103,355,228,357,229,356,230,358,231,
    359,360,232,361,362,366,233,363,110,111,112,113,114,109,240,364,234,365,115,367,116,368,117,118,369,119,120,121,122,123,
    124,125,126,241,243,244,242,372,374,245,375,373,376,127,246,377,128,129,247,378,371,370,248,249,379,130,250,251,131,132,
    381,382,252,253,380,133,134,383,384,135,254,136,137,255,256,257,258,259,260,261,385,387,388,386,262,389,391,263,264,390,
    392,393,265,395,394,266,396,267,140,139,141,142,143,397,398,432,144,269,138,145,433,434,399,268,146,435,147,148,149,400,
    436,271,270,272,273,150,151,443,437,274,401,402,403,404,405,152,153,444,154,438,156,445,439,440,441,275,454,406,276,407,
    155,277,278,446,408,279,280,158,410,281,282,409,157,159,411,160,161,412,413,162,447,455,283,285,286,414,284,416,417,415,
    287,163,288,289,290,448,456,164,291,165,418,420,292,449,452,450,451,461,293,166,419,421,457,294,422,424,167,458,423,295,
    425,296,426,427,297,459,428,298,429,460,168,299,430,169,300,431,442,462,453,463,464]

SCRATCH = {
    "x0": ("sbuf", [128, W], "int32"), "tt": ("sbuf", [128, W], "int32"), "ti": ("sbuf", [128, W], "int32"),
    "stb": ("sbuf", [128, W // 16], "int32"), "indb": ("sbuf", [128, 8], "bfloat16"), "indf": ("sbuf", [128, 8], "float32"),
    "sg": ("sbuf", [128, 8], "float32"), "sc": ("sbuf", [128, 1], "float32"), "cab": ("sbuf", [128, 3], "float32"),
    "eyeb": ("sbuf", [128, 128], "bfloat16"), "dm": ("sbuf", [128, 128], "bfloat16"), "sr": ("sbuf", [128, 2048], "bfloat16"),
    "bs": ("sbuf", [128, L], "bfloat16"), "bc": ("sbuf", [128, N], "bfloat16"), "cv": ("sbuf", [128, 128 * RH], "bfloat16"),
    "oh": ("sbuf", [128, W // 16], "float16"), "ob": ("sbuf", [128, W // 16], "float32"), "oc": ("sbuf", [128, W // 16], "float32"),
    "pf0": ("psum", [128, 512], "float32"), "pf1": ("psum", [128, 512], "float32"),
}
for _q in range(NC):
    for _k, _s, _d in (("off", [128, L], "uint16"), ("rc", [128, RO * NR * L], "float32"),
                       ("xx", [128, 2 * L], "float32"), ("mx", [128, L], "float32"), ("pc", [128, RO, 5 * L], "float16"),
                       ("lt", [128, 128], "float16"), ("gt", [128, N], "float32"), ("cm", [128, N], "bfloat16"),
                       ("ga", [128, N], "float32"), ("cc", [128, N], "bfloat16"), ("pp", [128, N], "float32"),
                       ("hf", [128, RO * L], "bfloat16"), ("hv", [128, 2 * RO * L], "float16"), ("fa", [128, 128], "float16"),
                       ("fb", [128, 256], "float16"), ("oo", [128, 2 * L], "float32"),
                       ("yp", [128, 2 * L], "float16"), ("ft", [128, 128], "float16")):
        SCRATCH["%s%d" % (_k, _q)] = ("sbuf", _s, _d)
    SCRATCH["pv%d" % _q] = ("psum", [128, 512], "float32")
    SCRATCH["po%d" % _q] = ("psum", [128, 512], "float32")

SHARE = {"ct0": "va", "ca0": "va", "mu0": "va", "ct1": "vb", "ca1": "vb", "mu1": "vb", "pn0": "ta", "dd0": "ta", "ps0": "ta",
         "pn1": "tc", "dd1": "tc", "ps1": "tc", "pt": "tp", "pb": "tp", "e3": "tp", "e5": "tp", "xx": "vx", "lo": "vx", "s0": "vx",
         "ev": "so", "of": "so", "ob": "so", "e1": "vo", "e2": "vo", "e6": "vo", "hv": "vh",
         "sn": "th", "h1": "th", "h3": "th", "hf": "sh", "h2": "sh", "h4": "sh", "e4": "sh"}


def build():
    ops, lastw, readers, bank = [], {}, {}, {}

    def op(queue, sem, emit, reads, writes, ninc=1, after=(), banks=(), order=()):
        n = len(ops)
        if sem is not None and sem[:-1] in SHARE:
            sem = SHARE[sem[:-1]] + sem[-1]
        o = {"n": n, "q": queue, "sem": sem, "emit": emit, "ninc": ninc, "deps": set(after), "order": set(order)}
        for t in reads:
            if t in lastw:
                o["deps"].add(lastw[t])
        for t in writes:
            if t in lastw:
                o["deps"].add(lastw[t])
            o["deps"].update(readers.get(t, ()))
        for t in reads:
            readers.setdefault(t, set()).add(n)
        for t in writes:
            lastw[t] = n
            readers[t] = set()
        for b in banks:
            acc = bank.get(b, [])
            o["deps"].update(i for i in acc if ops[i]["q"] != queue)
            o["order"].update(i for i in acc if ops[i]["q"] == queue)
            bank[b] = (acc if any(ops[i]["q"] == queue for i in acc) else []) + [n]
        o["deps"].discard(n)
        o["order"] -= o["deps"]
        ops.append(o)
        return n

    A = AluOpType
    F = ActivationFunctionType
    CPY = F.Copy
    V, S, P, G = "vector", "scalar", "tensor", "gpsimd"
    ls = op("sync", "l_st", lambda g, T, x: [g.sync.dma_start(T.stb[:], T.st[:])], [], ["stb"], 16)
    zz = op(V, "c_z", lambda g, T, x: [g.vector.memset(T.sr[:, 0:512], 0.0)], [], ["sra"])
    za = op(V, "c_x0", lambda g, T, x: [g.vector.memset(T.x0[:, 0:ZV], 0)], [], [], order=(zz,))
    zb = op(S, "c_x1", lambda g, T, x: [g.scalar.activation(T.x0[:, ZV:ZS], T.sr[:, 0:ZS - ZV], CPY)], ["sra"], [])
    zc = op(G, "c_x2", lambda g, T, x: [g.iota(T.x0[:, ZS:W], [[0, W - ZS]], 0, 0)], [], [])
    l0 = op("sync", "l_x0", lambda g, T, x: [g.sync.dma_start(T.x0[0:128:16, :], T.ids[0:128:16, :])], [], ["x0"], 16, after=(za, zb, zc), order=(ls,))
    l1 = op("sync", "l_tt", lambda g, T, x: [g.sync.dma_start(T.tt[:], T.tops[:])], [], ["tt"], 16, order=(l0,))
    op("sync", "l_ti", lambda g, T, x: [g.sync.dma_start(T.ti[:], T.ids[:])], [], ["ti"], 16, order=(l1,))
    op(V, "c_m1", lambda g, T, x: [g.vector.memset(T.indb[:], 1.0)], [], ["indb"])
    op(V, "c_m2", lambda g, T, x: [g.vector.memset(T.eyeb[:], 0.0)], [], ["eyeb"])
    op(V, "c_m3", lambda g, T, x: [g.vector.memset(T.bs[:], 0.0)], [], ["bs"])
    op(V, "c_m4", lambda g, T, x: [g.vector.memset(T.sr[:, 512:2048], 0.0)], [], ["srb"])
    op(V, "c_m5", lambda g, T, x: [g.vector.memset(T.dm[:], 0.0)], [], ["dm"])
    op(V, "c_m6", lambda g, T, x: [g.vector.memset(T.sg[:], 1.0)], [], ["sg"])
    op(V, "c_m7", lambda g, T, x: [g.vector.memset(T.cab[64 * h:64 * h + 64, c:c + 1], v) for h, c, v in (
        (0, 0, 1.0), (1, 0, -0.3125), (0, 1, 0.0), (1, 1, 0.125), (0, 2, 32.0), (1, 2, 1.0))], [], ["cab"], 6)
    op(V, "c_m11", lambda g, T, x: [g.vector.memset(T.cv[:], 0.0)], [], ["cv"])

    def sel(name, buf, sl, pat, cmp, fill, base, cm=1):
        op(G, name, lambda g, T, x: [g.affine_select(T[buf][:, sl], T[buf][:, sl], pat, cmp, fill, base, cm)], [buf], [buf])
    full = slice(0, 8)
    sel("c_i1", "indb", full, [[-16, 8]], A.is_ge, 0.0, 0)
    sel("c_i2", "indb", full, [[16, 8]], A.is_ge, 0.0, 15, -1)
    sel("c_ey", "eyeb", slice(0, 128), [[-1, 128]], A.not_equal, 1.0, 0)
    for pz in range(128 // L):
        sel("c_b%d" % pz, "bs", slice(0, L), [[-1, L]], A.not_equal, 1.0, -L * pz)
    sel("c_sg", "sg", full, [[-16, 8]], A.not_equal, -1.0, -15)
    sel("c_d1", "dm", slice(0, 128), [[-1, 128]], A.not_equal, -1.0, 0)
    sel("c_d2", "dm", slice(0, 128), [[-1, 128]], A.not_equal, 1.0, 1)
    sel("c_d3", "dm", slice(0, 128, 16), [[-16, 8]], A.not_equal, 0.0, 1)
    sel("c_d4", "dm", slice(0, 128, 16), [[-16, 8]], A.not_equal, 1.0, -15)
    sel("c_d5", "dm", slice(15, 128, 16), [[-16, 8]], A.not_equal, 0.0, -15)
    sel("c_d6", "dm", slice(15, 128, 16), [[-16, 8]], A.not_equal, -1.0, -14)
    op(V, "c_sc", lambda g, T, x: [g.vector.tensor_reduce(T.sc[:], T.sg[:], AxisListType.X, A.min)], ["sg"], ["sc"])
    op(S, "c_if", lambda g, T, x: [g.scalar.activation(T.indf[:], T.indb[:], CPY, scale=0.03125)], ["indb"], ["indf"])

    def mksr(g, T, x):
        return [g.scalar.activation(T.sr[:, 128 * r + r:128 * r + 128:16], T.indb[:], CPY) for r in range(16)]
    op(S, "c_sr", mksr, ["indb"], ["sra", "srb"], 16)

    def mkbc(g, T, x):
        return [g.vector.tensor_scalar(T.bc[:, i:N:16], T.bs[:], T.cab[:, 2:3], None, A.mult) for i in range(16)]
    op(V, "c_bc", mkbc, ["bs", "cab"], ["bc"], 16)
    for h in range(RH):
        def mkcv(g, T, x, h=h):
            return [g.scalar.activation(T.cv[:, h * 128 + NK * h + k:h * 128 + 128:16], T.bs[:, 8 * k:8 * k + 8], CPY) for k in range(NK)]
        op(S, "c_cv%d" % h, mkcv, ["bs", "cv"], ["cv_%d" % h], NK)
    CV = ["cv_%d" % h for h in range(RH)]
    op(V, "c_ob", lambda g, T, x: [g.vector.tensor_copy(T.oh[:], T.stb[:])], ["stb"], ["oh%d" % q for q in range(NC)])

    def conv(o, parts):
        def f(g, T, x):
            steps = [(b, c, n, h) for b, c, n in parts for h in range(RH)]
            return [g.tensor.matmul(o(T), T.cv[0:n, 128 * h:128 * h + 128], T[b][0:n, c + h:c + 128:RH], i == 0, i == len(steps) - 1)
                    for i, (b, c, n, h) in enumerate(steps)]
        return f

    def hits(q, ra, pf):
        Z = str(q)
        n = str(ra)

        def sn(g, T, x):
            return [g.tensor.matmul(T[pf][:, 256 + r * L:256 + r * L + L], T.eyeb[:], T["pc" + Z][:, r, z * L:z * L + L], z == 2, z == 4)
                    for r in (ra, ra + 1) for z in (2, 3, 4)]
        op(P, "sn" + Z, sn, ["pc%d_%d_n" % (q, r) for r in (ra, ra + 1)] + ["eyeb"], [], 6, banks=[pf])
        s = slice(ra * L, ra * L + 2 * L)
        op(S, "hf" + Z, lambda g, T, x: [g.scalar.activation(T["hf" + Z][:, s], T[pf][:, 256 + ra * L:256 + ra * L + 2 * L], F.Relu, bias=0.25, scale=-0.25)],
           [], ["hf" + n + Z], banks=[pf])

        def hv(g, T, x):
            return [g.vector.tensor_tensor(T["hv" + Z][:, (2 * r + a) * L:(2 * r + a) * L + L], T["pc" + Z][:, r, a * L:a * L + L],
                                           T["hf" + Z][:, r * L:r * L + L], A.mult) for r in (ra, ra + 1) for a in (0, 1)]
        op(V, "hv" + Z, hv, ["pc%d_%d_%s" % (q, r, t) for r in (ra, ra + 1) for t in "hl"] + ["hf" + n + Z], ["hv" + n + Z], 4)

    def chunk(q):
        cols = slice(L * q, L * q + L)
        Z = str(q)
        PV, PO = "pv" + Z, "po" + Z
        H = N // 2

        def nm(*a):
            return [k + Z for k in a]

        op(V, "oi" + Z, lambda g, T, x: [g.vector.tensor_copy(T["off" + Z][:], T.stb[:, cols])], ["stb"], nm("off"))
        if q % 2 == 0:
            op(S, "g0" + Z, lambda g, T, x: [g.scalar.activation(T["pp" + Z][:], T.x0[:, 0:W].indirect(T["off" + Z][:, 0:L]), CPY)],
               ["x0"] + nm("off"), nm("ppA", "ppB"))
        else:
            op(V, "g0" + Z, lambda g, T, x: [g.vector.tensor_copy(T["pp" + Z][:], T.x0[:, 0:W].indirect(T["off" + Z][:, 0:L]))],
               ["x0"] + nm("off"), nm("ppA", "ppB"))

        def sums():
            for a, t in ((0, "ppA"), (1, "ppB")):
                def f(g, T, x, a=a):
                    return [g.tensor.matmul(T[PV][:, 8 * k:8 * k + 8], T["pp" + Z][:, k:N:NK], T.indf[:], True, True) for k in range(a, NK, 2)]
                op(P, "ps%d" % a + Z, f, nm(t) + ["indf"], [], NK // 2, banks=[PV])

        def rc(T, r, a, b):
            return T["rc" + Z][:, (r * NR + a) * L:(r * NR + b) * L]

        def send(r):
            sums()

            def s0(g, T, x):
                o, i = rc(T, r, x["rank"], x["rank"] + 1), T[PV][:, 0:L]
                if x["rank"] == 1:
                    return [g.vector.tensor_scalar(o, i, (END - 0.25) / 32.0, None, A.min)]
                return [g.vector.tensor_copy(o, i)]
            op(V, "s0" + Z, s0, [], ["own%d_%d" % (q, r)], banks=[PV])

            def ex(g, T, x):
                s = rc(T, r, x["rank"], x["rank"] + 1)
                tr = [RemoteDMATransfer(dst_ids=[DstId(rid=a[0], pnc=a[1])], dma_engine_mask=m, remote_sem=T.sem["ar%d_%d" % (q, r)],
                                        srcs=[s], dsts=[s], alu_op=0) for a, m in x["peers"]]
                g.remote_dma_fused(tr, local_sem=T.sem["sent"])
                return []
            k = op(G, None, ex, ["own%d_%d" % (q, r)], [], 0)
            op("remote", "ar%d_%d" % (q, r), None, [], ["arr%d_%d" % (q, r)], 0, after=(k,))

        send(0)
        for r in range(RO):
            op(S, "gt" + Z, lambda g, T, x: [g.scalar.activation(T["gt" + Z][:], T.tt[:, 0:W].indirect(T["off" + Z][:, 0:L]), CPY)],
               ["tt"] + nm("off"), nm("gt"))
            src = ["arr%d_%d" % (q, r), "own%d_%d" % (q, r)]
            mx = lambda T: T["mx" + Z][:]
            pc = lambda T, a, b, r=r: T["pc" + Z][:, r, a * L:b * L]
            xh = lambda T: (T["xx" + Z][:, 0:L], T["xx" + Z][:, L:2 * L])
            pt = "pc%d_%d_" % (q, r)
            op(V, "xx" + Z, lambda g, T, x, r=r: [g.vector.tensor_tensor(T["xx" + Z][:], rc(T, r, 0, 2), rc(T, r, 2, 4), A.max)], src, nm("xx"))
            op(V, "ne" + Z, lambda g, T, x, r=r, pc=pc: [g.vector.tensor_tensor(pc(T, 2, 5), rc(T, r, 0, 3), rc(T, r, 1, 4), A.not_equal)], src, [pt + "n"])
            op(V, "mx" + Z, lambda g, T, x, mx=mx: [g.vector.tensor_tensor(mx(T), xh(T)[0], xh(T)[1], A.max)], nm("xx"), nm("mx"))
            op(V, "hi" + Z, lambda g, T, x, pc=pc: [g.vector.tensor_tensor(pc(T, 0, 1), xh(T)[0], xh(T)[1], A.max)], nm("xx"), [pt + "h"])
            op(V, "lo" + Z, lambda g, T, x, mx=mx, pc=pc: [g.vector.tensor_tensor(pc(T, 1, 2), mx(T), pc(T, 0, 1), A.subtract)],
               nm("mx") + [pt + "h"], [pt + "l"])

            def tp(g, T, x, pc=pc):
                return [g.tensor.matmul(T[PO][0:3 * L, 0:128], pc(T, 0, 3), T.eyeb[:], True, True),
                        g.tensor.matmul(T[PO][3 * L:4 * L, 0:128], pc(T, 3, 4), T.eyeb[:], True, False),
                        g.tensor.matmul(T[PO][3 * L:4 * L, 0:128], pc(T, 4, 5), T.eyeb[:], False, True)]
            op(P, "pt" + Z, tp, [pt + "h", pt + "l", pt + "n", "eyeb"], [], 3, banks=[PO])
            op(S, "ev" + Z, lambda g, T, x: [g.scalar.activation(T["lt" + Z][:], T[PO][:, 0:128], F.Identity, bias=T.cab[:, 1:2], scale=T.cab[:, 0:1])],
               ["cab"], nm("lt"), banks=[PO])
            op(P, "pb" + Z, lambda g, T, x: [
                g.tensor.matmul(T[PV][:, k:N:NK], T.bc[:, 128 * k:128 * k + 128], T["lt" + Z][:], True, True) for k in range(NK)],
               nm("lt") + ["bc"], [], NK, banks=[PV])
            pn = lambda T: T[PO][:, 384:384 + L]
            op(P, "bm" + Z, lambda g, T, x, pn=pn: [g.tensor.matmul(pn(T), T.eyeb[:], T.oh[:, cols], True, False)],
               nm("oh") + ["eyeb"], [], banks=[PO])
            for a in (0, 1):
                op(V, "ct%d" % a + Z, lambda g, T, x, a=a: [
                    g.vector.tensor_tensor(T["cm" + Z][:, a:N:2], T["gt" + Z][:, a:N:2], T[PV][:, a:N:2], A.is_lt)], nm("gt"), nm("cm%d" % a), banks=[PV])
            for a in (0, 1):
                def cnt(g, T, x, a=a, pn=pn):
                    return [g.tensor.matmul(pn(T), T.sr[:, 128 * i:128 * i + 128], T["cm" + Z][:, i:N:16], False, i == 15) for i in range(a, 16, 2)]
                op(P, "pn%d" % a + Z, cnt, nm("cm%d" % a) + ["sra", "srb"], [], 8, banks=[PO])
            op(S, "of" + Z, lambda g, T, x, pn=pn: [g.scalar.activation(T["off" + Z][:], pn(T), CPY)], [], nm("off"), banks=[PO])
            to = "oh" if r < RO - 1 else "ob"
            op(S, "ob" + Z, lambda g, T, x, pn=pn, to=to: [g.scalar.activation(T[to][:, cols], pn(T), CPY)], [], nm(to), banks=[PO])
            for a in (0, 1):
                def gx(g, T, x, a=a):
                    return [g.scalar.activation(T["ga" + Z][:, a * H:a * H + H], T.ti[:, 0:W].indirect(T["off" + Z][:, a * L // 2:a * L // 2 + L // 2]), CPY, scale=T.sc[:])]
                op(S, "ga%d" % a + Z, gx, ["ti", "sc"] + nm("off"), nm("ga%d" % a))
            for a in (0, 1):
                h = slice(a * H, a * H + H)
                op(V, "ca%d" % a + Z, lambda g, T, x, h=h: [
                    g.vector.tensor_tensor(T["cc" + Z][:, h], T["ga" + Z][:, h], T[PV][:, h], A.is_lt)], nm("ga%d" % a), nm("cc%d" % a), banks=[PV])
                op(P, "dd%d" % a + Z, lambda g, T, x, h=h: [g.tensor.matmul(T[PO][:, h], T.dm[:], T["cc" + Z][:, h], True, True)],
                   nm("cc%d" % a) + ["dm"], [], banks=[PO])
            for a, t in ((0, "ppA"), (1, "ppB")):
                op(V, "mu%d" % a + Z, lambda g, T, x, a=a: [
                    g.vector.tensor_tensor(T["pp" + Z][:, a:N:2], T["ga" + Z][:, a:N:2], T[PO][:, a:N:2], A.mult)], nm("ga0", "ga1"), nm(t), banks=[PO])
            if r < RO - 1:
                send(r + 1)
            if r == 1:
                hits(q, 0, "pf0")
                op(P, "h1" + Z, lambda g, T, x: [g.tensor.matmul(T.pf0[:, 0:128], T["hv" + Z][:, 0:128], T.eyeb[:], True, True)],
                   nm("hv0") + ["eyeb"], [], banks=["pf0"])
                op(S, "h2" + Z, lambda g, T, x: [g.scalar.activation(T["fa" + Z][:], T.pf0[:, 0:128], CPY)], [], nm("fa"), banks=["pf0"])
        sums()
        op(V, "e1" + Z, lambda g, T, x: [g.vector.tensor_copy(T["yp" + Z][:, 0:L], T[PV][:, 0:L])], [], nm("ypa"), banks=[PV])
        op(V, "e2" + Z, lambda g, T, x: [g.vector.tensor_tensor(T["yp" + Z][:, L:2 * L], T[PV][:, 0:L], T["yp" + Z][:, 0:L], A.subtract)],
           nm("ypa"), nm("ypb"), banks=[PV])
        op(P, "e3" + Z, lambda g, T, x: [g.tensor.matmul(T[PO][0:2 * L, 0:128], T["yp" + Z][:], T.eyeb[:], True, True)],
           nm("ypa", "ypb") + ["eyeb"], [], banks=[PO])
        op(S, "e4" + Z, lambda g, T, x: [g.scalar.activation(T["ft" + Z][0:2 * L, :], T[PO][0:2 * L, 0:128], CPY)], [], nm("ft"), banks=[PO])
        op(P, "e5" + Z, conv(lambda T: T[PO][:, 384:384 + L], [("ft" + Z, 0, 2 * L)]), nm("ft") + CV, [], RH, banks=[PO])
        op(V, "e6" + Z, lambda g, T, x: [g.vector.tensor_scalar(T.oc[:, cols], T[PO][:, 384:384 + L], 32.0, None, A.mult)], [], nm("oc"), banks=[PO])

    def last(q):
        cols = slice(L * q, L * q + L)
        Z = str(q)
        hits(q, 2, "pf0")
        op(P, "h1" + Z, lambda g, T, x: [g.tensor.matmul(T.pf1[:, 0:128], T["hv" + Z][:, 128:256], T.eyeb[:], True, True),
                                         g.tensor.matmul(T.pf1[:, 128:256], T["hf" + Z][:], T.eyeb[:], True, True)],
           ["hv2" + Z, "hf0" + Z, "hf2" + Z, "eyeb"], [], 2, banks=["pf1"])
        op(S, "h2" + Z, lambda g, T, x: [g.scalar.activation(T["fb" + Z][:], T.pf1[:, 0:256], CPY)], [], ["fb" + Z], banks=["pf1"])
        c1 = conv(lambda T: T.pf1[:, 384:384 + L], [("fa" + Z, 0, 128), ("fb" + Z, 0, 128)])
        c2 = conv(lambda T: T.pf1[:, 384 + L:384 + 2 * L], [("fb" + Z, 128, 128)])
        op(P, "h3" + Z, lambda g, T, x: c1(g, T, x) + c2(g, T, x), ["fa" + Z, "fb" + Z] + CV, [], 3 * RH, banks=["pf1"])
        op(S, "h4" + Z, lambda g, T, x: [g.scalar.activation(T["oo" + Z][:, 0:L], T.pf1[:, 384:384 + L], CPY, scale=128.0),
                                         g.scalar.activation(T["oo" + Z][:, L:2 * L], T.pf1[:, 384 + L:384 + 2 * L], CPY, scale=4.0)],
           [], ["oo" + Z], 2, banks=["pf1"])
        for y, src, tok in (("yb", lambda T: T.ob[:, cols], "ob"), ("ys", lambda T: T["oo" + Z][:, 0:L], "oo"),
                            ("yh", lambda T: T["oo" + Z][:, L:2 * L], "oo"), ("yc", lambda T: T.oc[:, cols], "oc")):
            op("sync", "out", lambda g, T, x, y=y, src=src: [g.sync.dma_start(T[y][:, cols], src(T))], [tok + Z], [], 16)
    for q in range(NC):
        chunk(q)
    for q in range(NC):
        last(q)
    return ops


def plan():
    ops, order = build(), SEQ
    pos = {i: z for z, i in enumerate(order)}
    assert len(pos) == len(ops) and all(pos[d] < pos[o["n"]] for o in ops for d in o["deps"] | o["order"])
    known, clos, waits, waited = {}, {}, {}, set()
    for i in order:
        o = ops[i]
        q = o["q"]
        if q == "remote":
            clos[i] = 1 << i
            continue
        k = known.get(q, 0)
        ws = []
        for d in sorted(o["deps"], key=lambda d: -pos[d]):
            if not (k >> d) & 1:
                if ops[d]["ninc"] == 0 and ops[d]["q"] != "remote":
                    continue
                ws.append(d)
                k |= clos[d]
        ws = [d for d in ws if not any(e != d and (clos[e] >> d) & 1 for e in ws)]
        waits[i] = ws
        waited.update(ws)
        known[q] = k
        clos[i] = k | (1 << i)
    cnt, val = {}, {}
    for i in order:
        o = ops[i]
        if o["q"] != "remote" and o["sem"] is not None and (i in waited or o["sem"] == "out"):
            cnt[o["sem"]] = cnt.get(o["sem"], 0) + o["ninc"]
            val[i] = cnt[o["sem"]]
    return ops, order, waits, val, cnt


OPS, ORDER, WAITS, VAL, CNT = plan()
SEMAPHORES = sorted(CNT) + ["ar%d_%d" % (q, r) for q in range(NC) for r in range(RO)] + ["sent"]


def rank_program(g, core, T, topo):
    rank = T.rank_of(core)
    if rank is None:
        return
    peers = [c for c in T.cores if c != core]
    chip = topo.cores_of(core)
    far = [c for c in peers if c not in chip]
    near = [c for c in peers if c in chip]
    masks = {}
    used = []
    for i, c in enumerate(far):
        e = topo.engines(core, c)
        e = e[i * (len(e) // len(far)):(i + 1) * (len(e) // len(far))]
        used += e
        masks[c] = e
    for i, c in enumerate(near):
        e = [k for k in topo.engines(core, c) if k not in used][4 * i:4 * i + 4]
        masks[c] = e
    inn = sum(len(masks[c]) for c in peers)
    x = {"rank": rank, "peers": [(topo.addr(c, core), sum(1 << k for k in masks[c])) for c in far + near]}
    queue = {"sync": g.sync, "scalar": g.scalar, "vector": g.vector, "tensor": g.tensor, "gpsimd": g}
    sends = 0
    for i in ORDER:
        o = OPS[i]
        if o["q"] == "remote":
            continue
        e = queue[o["q"]]
        for d in WAITS[i]:
            p = OPS[d]
            e.wait_ge(T.sem[p["sem"]], inn if p["q"] == "remote" else VAL[d])
        ins = o["emit"](g, T, x)
        if o["sem"] is None:
            sends += 1
        if i in VAL:
            for k in ins:
                k.then_inc(T.sem[o["sem"]], o["ninc"] // len(ins))
    g.sync.wait_ge(T.sem["out"], CNT["out"])
    g.wait_ge(T.sem["sent"], inn * sends)
